import numpy as np, ml_dtypes
CORES = [2,6,10,14,18,22,26,30]
N = 8
import mx_ref
BF = ml_dtypes.bfloat16
def gentries(a):
    return np.ascontiguousarray(a.reshape(8, 16, -1).transpose(0, 2, 1)).reshape(8, -1)
def gtable(e):
    e = np.asarray(e); return np.ascontiguousarray(e.reshape(8, -1, 16).transpose(0, 2, 1)).reshape(128, -1).astype(np.int32)
def gcols(t, e):
    v = np.concatenate([t.reshape(8, 16, -1, 4), np.zeros((8, 16, 1, 4), BF)], axis=2)
    return np.ascontiguousarray(np.stack([v[g][:, e[g]] for g in range(8)])).reshape(128, -1)
def tile(rs):
    return np.stack(rs, axis=2).reshape(128, -1).astype(BF)
def pick(q, e):
    c = np.concatenate([q[0].reshape(128, -1, 4), np.zeros((128, 1, 4), np.uint8)], axis=1); s = np.concatenate([q[1], np.ones((16, 1), np.uint8)], axis=1)
    return (np.ascontiguousarray(c[:, e].reshape(128, -1)), np.ascontiguousarray(s[:, e]))
def join(*qs):
    return (np.concatenate([q[0] for q in qs], axis=1), np.concatenate([q[1] for q in qs], axis=1))
def put(q, e, v):
    c, s = q[0].reshape(128, -1, 4).copy(), q[1].copy(); c[:, e] = v[0].reshape(128, -1, 4); s[:, e] = v[1]
    return (c.reshape(128, -1), s)
def pk(c, s):
    return (np.ascontiguousarray(c), mx_ref.live(s))
def emit(q):
    return q[0], q[1]
def packed(v, rng):
    q = [mx_ref.quantize(np.ascontiguousarray(v[r])) for r in range(N)]
    return np.stack([a for a, b in q]), np.stack([mx_ref.plane(b, rng) for a, b in q])
def values_of_codes():
    e, c = np.zeros((128, 128, 4), np.float32), np.zeros((128, 2, 4), np.uint8)
    e[np.arange(128), np.arange(128), 0] = 1
    c[:127, :, 0] = np.arange(256).reshape(2, 128).T[:127]
    return mx_ref.matmul(mx_ref.quantize(e.reshape(128, 512).astype(BF)), (c.reshape(128, 8), np.full((16, 2), 127, np.uint8))).T.reshape(-1).astype(np.float64)
CODE_VALUE, SCALE_VALUE = values_of_codes(), 2.0 ** (np.arange(256) - 127.0)
def decode(q):
    return (CODE_VALUE[q[0]].reshape(16, 8, -1, 4) * SCALE_VALUE[q[1]][:, None, :, None] + 0.0).reshape(128, -1).astype(np.float32)
def f(rng, *shape):
    return mx_ref.flush((rng.standard_normal(shape, dtype=np.float32) * np.exp2(rng.integers(-2, 3, shape[:-1] + (1,)))).astype(BF))
def wide(rng, *shape, cols=0):
    v = rng.standard_normal(shape, dtype=np.float32) * np.exp2(rng.integers(-12, 13, shape)).astype(np.float32)
    if cols: v *= np.repeat(np.exp2(rng.integers(-cols, cols + 1, shape[:-2] + (1, shape[-1] // 4))) * (rng.random(shape[:-2] + (1, shape[-1] // 4)) > 0.0625), 4, axis=-1).astype(np.float32)
    return mx_ref.flush(v.astype(BF))
C = 256
STEP = [1, 2, 4]
HOPS = 128
def numbers_of(rng):
    return {"x": np.array(f(rng, N, 128, 4 * C)), "u": np.array(f(rng, N, 128, 512)), "v": np.array(f(rng, N, 128, 512))}
def orders(rng):
    e = np.tile(np.arange(C), (N, 8, 1))
    k, a, t = rng.permuted(e, axis=2), rng.permuted(e, axis=2)[:, :, 16:], e.copy()
    np.put_along_axis(t, a[:, :, 0::2], a[:, :, 1::2], axis=2)
    np.put_along_axis(t, a[:, :, 1::2], a[:, :, 0::2], axis=2)
    return k, t
def stored(k, t):
    return {"nx": np.stack([gtable(k[r]) for r in range(N)]), "mt": np.stack([gtable(t[r]) for r in range(N)])}
def layers(rng, still=[]):
    w = np.array(f(rng, N, 128, 2048)).reshape(N, 8, 16, 4, 8, 16, 4)
    for i in still:
        w[:, :, i] = 0
        w[:, :, :, :, :, i] = 0
    return w
def weights(rng, w):
    c, p = packed(np.ascontiguousarray(w).reshape(N, 128, 2048), rng)
    return {"wc": c, "ws": p}
def setup_inputs(rng):
    return {**numbers_of(rng), **stored(*orders(rng)), **weights(rng, layers(rng))}
def setup_inputs_ties(rng):
    d = numbers_of(rng)
    k, t = orders(rng)
    o = rng.permutation(N) % 4
    n = rng.integers(0, 4, (N, 8, C))
    c = np.ones((N, 8), np.float32)
    for r in range(N):
        c[r] = rng.permutation(8) % 2 * 2.0 - 1.0
        for g in range(8):
            if o[r] < 2:
                e = rng.permutation(C)
                a = np.arange(C) + 1 if c[r, g] < 0 else C - np.arange(C)
                n[r, g, e] = a if o[r] == 0 else (a + 1) // 2
                k[r, g, e] = np.roll(e, -1)
            if o[r] == 3: n[r, g] = rng.integers(0, 2, C) if g % 2 else 1
        if o[r] < 2: t[r, rng.permutation(8)[:4]] = np.arange(C)
    digits = (n[..., None] & (1 << np.arange(12))).reshape(N, 8, C, 3, 4)
    x = d["x"].reshape(N, 8, 16, C, 4)
    x[:, :, 8:] = 0
    x[:, :, 8:11] = digits.transpose(0, 1, 3, 2, 4).astype(np.float32).astype(BF)
    u = d["u"].reshape(N, 128, 128, 4)
    u[:, :, ::16] = 0
    for g in range(8): u[:, 16 * g + 8:16 * g + 11, 16 * g] = c[:, g].astype(BF)[:, None, None]
    w = layers(rng)
    w[:, :, :, :, :, 8:] = 0
    return {"x": x.reshape(N, 128, 4 * C), "u": u.reshape(N, 128, 512), "v": d["v"], **stored(k, t), **weights(rng, w)}
def setup_inputs_near(rng):
    d = numbers_of(rng)
    x = d["x"].astype(np.float32).reshape(N, 8, 16, C, 4)
    x[:, :, :2] = 0
    x[:, :, 8:] = 0
    u = d["u"].reshape(N, 128, 128, 4)
    u[:, :, ::16] = 0
    w = layers(rng, [0, 1, 8, 9, 10, 11, 12, 13, 14, 15])
    o = (np.arange(N) + rng.integers(N)) % 4
    for r in range(N):
        c = rng.choice([-1.0, 1.0], (8, 1))
        s = rng.integers(0, 16, (8, C))
        digits = ((s[:, :, None] >> np.arange(4)) & 1) * np.exp2(np.arange(4) - 23.0)
        if o[r] < 2:
            x[r, :, 0, :, 0] = c
            x[r, :, 8] = digits
            x[r, :, 11, :, 0] = 2.0 ** -10
        else:
            x[r, :, :8] = 0
            x[r, :, 13, :, 0] = 2.0 ** -30
            x[r, :, 1, :, 0] = rng.choice([-1.0, 1.0], (8, C)) * 2.0 ** -30
            w[r] = 0
            for g in range(8): w[r, g, 1, 0, g, 12, 0] = 2.0 ** -8
        if o[r] == 2: x[r, :, 8] = digits * rng.choice([-1.0, 1.0], (8, C, 1))
        if o[r] == 3:
            x[r, :, 8, :, 0] = np.where(s < 8, 1.25, 0.0) * 2.0 ** -30 * c
            x[r, :, 9, :, 0] = np.where(s < 8, 0.0, 1.125) * 2.0 ** -30 * c
            for g in rng.permutation(8)[:4]:
                e = rng.choice([-1.0, 1.0], C) * 2.0 ** -30
                x[r, g, 8, :, 0] = 1.25 * e
                x[r, g, 9, :, 0] = -1.125 * e
        at = [0, C - 1, int(rng.integers(C)), int(rng.integers(C))]
        for g, j in zip(rng.permutation(8)[:4], at): x[r, g, 0, j, 0] = 2.0 ** 29 * rng.choice([-1.0, 1.0])
        k = 1.0 if o[r] == 0 else 2.0 ** -30
        for h in range(0, 128, 16):
            u[r, h, h, 0] = k if o[r] < 2 else 1.0
            if o[r] < 2: u[r, h + 11, h, 0] = k
            if o[r] < 3: u[r, h + 8, h] = k
            else:
                u[r, h + 8, h, 0] = k
                u[r, h + 9, h, 0] = 1.125 * k
                u[r, h + 12, h, 0] = k
    return {"x": x.reshape(N, 128, 4 * C).astype(BF), "u": u.reshape(N, 128, 512), "v": d["v"], **stored(*orders(rng)), **weights(rng, w)}
def setup_inputs_odd(rng):
    d = numbers_of(rng)
    w = layers(rng, [0, 8])
    x = (1.0 + (2 * rng.integers(0, 64, (N, 16, 8, C, 4)) + 1) * 2.0 ** -7) * np.exp2(-rng.integers(0, 7, (N, 16, 8, C, 4)).astype(np.float64)) * rng.choice([-1.0, 1.0], (N, 16, 8, C, 4))
    x[:, 0::2, 0, :, 0] = 1.96875 * 2.0 ** 8 * rng.choice([-1.0, 1.0], (8, 1))
    x[:, 1::2, 0, :, 0] = rng.choice([1.96875 * 2.0 ** 8, 8.0], (N, 8, C)) * rng.choice([-1.0, 1.0], (N, 8, C))
    for g in range(8): w[:, g, 0, 0, g, 0, 0] = -0.5
    u = d["u"].reshape(N, 16, 8, 128, 4)
    u[:, :, 0, ::16] = 0
    for r in rng.permutation(N)[:N // 2]:
        for i, g in enumerate(rng.permutation(8)[:4]):
            x[r, 2 * g, 1, :, 0] = (8 + rng.integers(0, 2, C)) * 2.0 ** (i - 8)
            u[r, :, :, 16 * g] = 0
            u[r, 2 * g, 1, 16 * g, 0] = 1.0
            w[r, :, :, 0, g, 1] = 0
    return {"x": x.astype(np.float32).reshape(N, 128, 4 * C).astype(BF), "u": u.reshape(N, 128, 512), "v": d["v"], **stored(*orders(rng)), **weights(rng, w)}
def setup_inputs_ends(rng):
    d = numbers_of(rng)
    k, t = orders(rng)
    o, e, m = rng.permutation(N) % 4, rng.permutation(N) % 4, rng.permutation(N) % 4
    for r in range(N):
        s = (r - STEP[-1]) % N
        if o[r] == 3 and o[s] == 2:
            a = rng.choice([n for n in range(N) if o[n] < 2 and o[(n + STEP[-1]) % N] != 3])
            o[s] = o[a]
            o[a] = 2
    i = np.arange(C)
    k[e == 0] = i
    k[e == 1] = (i + 1) % C
    k[e == 2] = C - 1 - i
    k[e == 3] = (i - 1) % C
    t[m == 0] = i
    t[m == 1] = C - 1 - i
    t[m == 2] = i ^ 1
    x = np.zeros((N, 8, 16, C, 4))
    u = d["u"].astype(np.float32).reshape(N, 128, 128, 4)
    v = d["v"].astype(np.float32)
    w = np.zeros((N, 128, 4, 128, 4), np.float32)
    j = np.arange(128)
    for r in range(N):
        h = rng.permutation(8)
        c = np.where(h < 2, 0.0, h % 2 * 2.0 - 1.0)[None, :, None]
        low = -(0.7 + 0.1 * rng.random((8, 16, C, 4))) * 2.0 ** 30
        if o[r] == 0: x[r] = low
        if o[r] == 1: x[r] = low * rng.choice([-1.0, 1.0], (C, 1))
        if o[r] == 2: x[r] = -(1.0 + 0.125 * rng.integers(0, 8, (8, 16, C, 4))) * 2.0 ** -30
        if o[r] == 3: x[r] = d["x"][r].astype(np.float32).reshape(8, 16, C, 4)[:, :, :1]
        if o[r] < 2:
            u[r, :, ::16] = c * (0.9 + 0.1 * rng.random((128, 8, 4))) * 2.0 ** 30
            v[r] = rng.choice([-1.0, 1.0], (128, 512)) * (0.9 + 0.1 * rng.random((128, 512))) * 2.0 ** 30
        if o[r] == 2:
            u[r, :, ::16] = c * (1.0 + 0.125 * rng.integers(0, 8, (128, 8, 4))) * 2.0 ** -30
            v[r] = rng.choice([-1.0, 1.0], (128, 512)) * (1.0 + 0.125 * rng.integers(0, 8, (128, 512))) * 2.0 ** -30
        if o[r] == 3: u[r, :, ::16] *= np.abs(c).astype(np.float32)
        a = np.array([2.0, 2.0 ** -8, -0.25])[rng.permutation(8) % 3][j // 16]
        if o[r] == 2: a = np.zeros(128)
        a[120:] = 256.0
        for b in range(4): w[r, j, b, j, b] = a
    x[:, 7, 8:] = -2.0 ** -30
    return {"x": x.astype(np.float32).reshape(N, 128, 4 * C).astype(BF), "u": u.reshape(N, 128, 512).astype(BF), "v": v.astype(BF), **stored(k, t), **weights(rng, w.astype(BF))}
def setup_inputs_spread(rng):
    d = setup_inputs(rng)
    d["x"] = wide(rng, N, 128, 4 * C, cols=6)
    return d
def check_inputs(d):
    b = []
    for k in ("x", "u", "v"):
        a = np.abs(d[k].astype(np.float32))
        if not (np.isfinite(a).all() and ((a == 0) | (a >= 2.0 ** -30) & (a <= 2.0 ** 30)).all()): b.append("a value of " + k)
    none, least, most = [emit(mx_ref.quantize(np.full((128, 16), k, np.float32).astype(BF)))[1][0, 0] for k in (0.0, 2.0 ** -8, 2.0 ** 8)]
    for r in range(N):
        k, t = gentries(d["nx"][r]), gentries(d["mt"][r])
        if not (np.sort(k, axis=1) == np.arange(C)).all(): b.append("nx: not every column once")
        if not (((t >= 0) & (t < C)).all() and (np.take_along_axis(t, np.clip(t, 0, C - 1), axis=1) == np.arange(C)).all()): b.append("mt: not each other's")
        if ((d["wc"][r] == 0x7F) | (d["wc"][r] == 0xFF)).any(): b.append("wc: a code that is no number")
        s = mx_ref.live(d["ws"][r])
        if ((s != none) & ((s < least) | (s > most))).any(): b.append("ws: a scale out of range")
        if (((d["wc"][r].reshape(16, 8, 512, 4) & 0x7F) != 0) & (s == none)[:, None, :, None]).any(): b.append("wc: a code other than zero under the scale of zeros")
    return b
def at(a, e):
    return np.take_along_axis(a, e, axis=1)
def search(s, follow):
    b = np.tile(np.arange(C), (8, 1))
    p, left = b.copy(), np.ones((8, C), bool)
    for hop in range(1, HOPS + 1):
        to = at(follow, p)
        larger = left & (at(s, to) > s)
        b = np.where(larger, to, b)
        left = left & ~larger
        if hop < HOPS: p = np.where(left, to, p)
    return b, p
def layer(w, q):
    return tile([mx_ref.matmul(pick(w, np.arange(128 * k, 128 * k + 128)), q) * np.float32(0.03125) for k in range(4)])
def reference(x, u, v, nx, mt, wc, ws):
    qu = [mx_ref.quantize(u[r]) for r in range(N)]
    lay = [pk(wc[r], ws[r]) for r in range(N)]
    follow, mate = [gentries(nx[r]) for r in range(N)], [gentries(mt[r]) for r in range(N)]
    now = [x[r] for r in range(N)]
    for step in STEP:
        t, z, first = [], [], []
        for r in range(N):
            q = mx_ref.quantize(now[r])
            s = mx_ref.matmul(qu[r], q)[::16] + np.float32(0.0)
            b, p = search(s, follow[r])
            t.append(decode(q))
            c = t[r].astype(BF)
            z.append(mx_ref.quantize(((gcols(c, b).astype(np.float32) + gcols(c, p).astype(np.float32)) * np.float32(0.5)).astype(BF)))
            first.append(b)
            e = at(s, b)
            swap = at(e, np.minimum(mate[r], np.arange(C))) > at(e, np.maximum(mate[r], np.arange(C)))
            follow[r] = np.where(swap, at(follow[r], mate[r]), follow[r])
        now = [(t[r] + gcols(layer(lay[r], z[(r - step) % N]), first[r]).astype(np.float32)).astype(BF) for r in range(N)]
    y, nf = np.zeros((N, 128, C), np.float32), np.zeros((N, 8, C), np.float32)
    oc, osc = np.zeros((N, 128, 4 * C), np.uint8), np.zeros((N, 16, C), np.uint8)
    for r in range(N):
        q = mx_ref.quantize(now[r])
        y[r] = mx_ref.matmul(mx_ref.quantize(v[r]), q)
        nf[r] = follow[r]
        oc[r], osc[r] = emit(q)
    return {"y": y, "nf": nf, "oc": oc, "osc": osc}

@@ -1,0 +1,465 @@
+from concourse.mybir import dt, AluOpType as A, ActivationFunctionType as F
+
+STEP = [1, 2, 4]
+C = 256
+R3 = 3
+CODE = "float8_e4m3fn_x4"
+SCRATCH = {
+    "ps": ("psum", [128, 4096], "float32"),
+    "ut": ("sbuf", [128, 512], "bfloat16"), "vt": ("sbuf", [128, 512], "bfloat16"),
+    "qu0": ("sbuf", [128, 128], CODE), "su0": ("sbuf", [128, 128], "uint8"),
+    "qu": ("sbuf", [128, 128], CODE), "su": ("sbuf", [128, 128], "uint8"),
+    "qv": ("sbuf", [128, 128], CODE), "sv": ("sbuf", [128, 128], "uint8"),
+    "wq": ("sbuf", [128, 512], CODE), "wp": ("sbuf", [128, 512], "uint8"),
+    "ones": ("sbuf", [128, 520], "bfloat16"), "et": ("sbuf", [128, 520], "bfloat16"),
+    "qe": ("sbuf", [128, 512], CODE), "se": ("sbuf", [128, 512], "uint8"),
+    "nxi": ("sbuf", [128, 16], "int32"), "mti": ("sbuf", [128, 16], "int32"),
+    "tj": ("sbuf", [128, 256], "float32"), "ii": ("sbuf", [128, 256], "float32"),
+    "idn": ("sbuf", [128, 256], "bfloat16"),
+    "pi": ("sbuf", [128, 8], "int32"), "qf": ("sbuf", [128, 8], "float32"), "inv": ("sbuf", [128, 8], "float32"),
+    "k16": ("sbuf", [128, 16], "float32"), "cw": ("sbuf", [128, 16], "float32"),
+    "d1": ("sbuf", [128, 256], "float32"), "d2": ("sbuf", [128, 256], "float32"),
+    "mka": ("sbuf", [128, 256], "float32"),
+    "mkf": ("sbuf", [128, 256], "float32"),
+    "dl": ("sbuf", [128, 256], "bfloat16"),
+    "lid": ("sbuf", [128, 16], "uint16"), "lu": ("sbuf", [128, 8], "uint16"), "lui": ("sbuf", [128, 8], "int32"),
+    "lm": ("sbuf", [128, 16], "uint16"), "lmin": ("sbuf", [128, 16], "uint16"), "lmax": ("sbuf", [128, 16], "uint16"),
+    "mf": ("sbuf", [128, 16], "float32"), "mmin": ("sbuf", [128, 16], "float32"), "mmax": ("sbuf", [128, 16], "float32"),
+    "sw": ("sbuf", [128, 256], "float32"), "s1": ("sbuf", [128, 256], "float32"), "s2": ("sbuf", [128, 256], "float32"),
+    "n6": ("sbuf", [128, 256], "bfloat16"), "nsc": ("sbuf", [128, 256], "bfloat16"),
+    "fm": ("sbuf", [128, 256], "bfloat16"), "fw": ("sbuf", [128, 16], "bfloat16"),
+    "sb": ("sbuf", [128, 256], "float32"), "xm": ("sbuf", [128, 256], "float32"),
+    "nff": ("sbuf", [128, 256], "float32"), "yt": ("sbuf", [128, 256], "float32"),
+    "fa": ("sbuf", [128, 1024], "bfloat16"), "fo": ("sbuf", [128, 1024], "bfloat16"),
+    "zg": ("sbuf", [128, 1024], "bfloat16"), "z": ("sbuf", [128, 1024], "bfloat16"), "hh": ("sbuf", [128, 1024], "bfloat16"),
+    "qz": ("sbuf", [128, 256], CODE), "sz": ("sbuf", [128, 256], "uint8"),
+    "vbz": ("sbuf", [128, 512], "bfloat16"),
+}
+for _i in range(2):
+    SCRATCH["mc%d" % _i] = ("sbuf", [128, 256], "float32")
+    for _n in ("cb", "vb", "rb"):
+        SCRATCH["%s%d" % (_n, _i)] = ("sbuf", [128, 512], "bfloat16")
+    SCRATCH["nb%d" % _i] = ("sbuf", [128, 256], "bfloat16")
+    SCRATCH["lw%d" % _i] = ("sbuf", [128, 16], "uint16")
+for _i in range(4):
+    SCRATCH["x%d" % _i] = ("sbuf", [128, 1024], "bfloat16")
+    SCRATCH["qx%d" % _i] = ("sbuf", [128, 256], CODE)
+    SCRATCH["sx%d" % _i] = ("sbuf", [128, 256], "uint8")
+for _i in range(3):
+    SCRATCH["lq%d" % _i] = ("sbuf", [128, 256], CODE)
+    SCRATCH["ls%d" % _i] = ("sbuf", [128, 256], "uint8")
+    for _n in ("lp", "lb", "zp", "zb"):
+        SCRATCH["%s%d" % (_n, _i)] = ("sbuf", [128, 16], "uint16")
+for _i in range(7):
+    SCRATCH["m%d" % _i] = ("sbuf", [128, 256], "float32")
+for _i in range(6):
+    SCRATCH["n%d" % _i] = ("sbuf", [128, 256], "bfloat16")
+    SCRATCH["l%d" % _i] = ("sbuf", [128, 16], "uint16")
+DMAS = ["dx", "dnx", "dmt", "du", "dwc", "dws", "dv", "doc", "dos0", "dos1", "dos2", "dos3", "dy0", "dy1", "dnf"]
+SEMAPHORES = ["cv", "cs", "ct", "cg", "sent"] + DMAS + ["%s%d" % (n, i) for n in ("arq", "arp", "arb", "arc") for i in range(3)]
+BIG = 1.0e29
+
+
+def make_issue(g, T):
+    queue = {"v": g.vector, "s": g.scalar, "t": g.tensor, "g": g, "y": g.sync}
+    known = {e: {} for e in queue}
+    count, clock, writer, readers = {}, {}, {}, {}
+
+    def learn(e, ev):
+        sem, val = ev
+        for s, n in list(clock.get(ev, {}).items()) + [(sem, val)]:
+            if known[e].get(s, 0) < n:
+                known[e][s] = n
+
+    def need(e, evs):
+        best = {}
+        for sem, val in evs:
+            if known[e].get(sem, 0) < val:
+                best[sem] = max(best.get(sem, 0), val)
+        evs = [(sem, val) for sem, val in best.items()]
+        for ev in evs:
+            if not any(o != ev and clock.get(o, {}).get(ev[0], 0) >= ev[1] for o in evs):
+                queue[e].wait_ge(T.sem[ev[0]], ev[1])
+        for ev in evs:
+            learn(e, ev)
+
+    def wait_for(e, reads=(), writes=()):
+        evs = []
+        for k in reads:
+            if k in writer:
+                evs.append(writer[k])
+            if k.startswith("ps"):
+                evs += [ev for ev, o in readers.get(k, []) if o != e]
+        for k in writes:
+            if k in writer:
+                evs.append(writer[k])
+            evs += [ev for ev, o in readers.get(k, [])]
+        need(e, evs)
+
+    def op(e, call, reads=(), writes=(), sem=None, inc=1):
+        wait_for(e, reads, writes)
+        sem = sem or "c" + e
+        call(queue[e]).then_inc(T.sem[sem], inc)
+        count[sem] = count.get(sem, 0) + inc
+        ev = (sem, count[sem])
+        clock[ev] = dict(known[e])
+        for k in reads:
+            readers.setdefault(k, []).append((ev, e))
+        for k in writes:
+            writer[k] = ev
+            readers[k] = []
+
+    def lands(key, sem, val):
+        writer[key] = (sem, val)
+        readers[key] = []
+
+    return op, wait_for, lands, count
+
+
+def rank_program(g, core, T, topo):
+    rank = T.rank_of(core)
+    if rank is None:
+        return
+    op, wait_for, lands, count = make_issue(g, T)
+    cores = T.cores
+    U8, U32 = dt.uint8, dt.uint32
+    sent = [0]
+
+    def few(src, dst):
+        return topo.engines(src, dst)[:8]
+
+    def send(dst, out, src, sem, reads):
+        wait_for("g", reads)
+        rid, pid = topo.addr(dst)[:2]
+        e = few(core, dst)
+        g.remote_dma(out, src, T.sem[sem], T.sem.sent, pid, rid, sum(1 << k for k in e))
+        sent[0] += len(e)
+
+    def V(call, reads, writes):
+        op("v", call, reads, writes)
+
+    def S(call, reads, writes):
+        op("s", call, reads, writes)
+
+    def both(name):
+        return [name + ".a", name + ".b"]
+
+    def bank(b, n=C):
+        return T.ps[:, 512 * b:512 * b + n]
+
+    def mm(b, stat, c0, mov, lo, n, reads):
+        (q, s), (x, y) = stat, mov
+        op("t", lambda e: e.matmul_mx(bank(b, n), T[q][:, c0:c0 + 128], T[s][:, c0:c0 + 128], T[x][:, lo:lo + n], T[y][:, lo:lo + n], True, True),
+           reads, ["ps%d" % b])
+
+    def quant(q, s, tile, key, reads, lo=0, n=128):
+        V(lambda v: v.quantize_mx(T[q][:, lo:lo + n], T[s][:, lo:lo + n], T[tile][:, 4 * lo:4 * lo + 4 * n]), reads, [key])
+
+    def pick(win, lst, a=0):
+        return T[win][:, a:a + C].indirect(T[lst][:, 0:16])
+
+    def half(win, lst, h):
+        return T[win][:, 0:C].indirect(T[lst][:, 8 * h:8 * h + 8])
+
+    op("y", lambda q: q.dma_start(T.nxi[:], T.nx[:]), [], ["nxi"], "dnx", 16)
+    op("s", lambda q: q.dma_start(T.x0[:], T.x[:]), [], ["x0"], "dx", 16)
+    op("y", lambda q: q.dma_start(T.ut[:], T.u[:]), [], ["ut"], "du", 16)
+    op("y", lambda q: q.dma_start(T.mti[:], T.mt[:]), [], ["mti"], "dmt", 16)
+    op("y", lambda q: q.dma_start(T.wq[:, 0:512].bitcast(U8), T.wc[:]), [], ["wq"], "dwc", 16)
+    op("y", lambda q: q.dma_start(T.wp[:, 0:512], T.ws[:]), [], ["wp"], "dws", 16)
+    op("y", lambda q: q.dma_start(T.vt[:], T.v[:]), [], ["vt"], "dv", 16)
+
+    op("g", lambda q: q.iota(T.pi[:, 0:1], [[0, 1]], 0, 1), [], ["pi"])
+    op("g", lambda q: q.iota(T.lui[:], [[16, 8]], 0, 0), [], ["lui"])
+    op("g", lambda q: q.iota(T.k16[:], [[16, 16]], 0, 0, allow_small_or_imprecise_dtypes=True), [], ["k16"])
+    op("g", lambda q: q.iota(T.tj[:], [[0, 16], [1, 16]], 0, 0, allow_small_or_imprecise_dtypes=True), [], ["tj"])
+    op("g", lambda q: q.iota(T.ii[:], [[1, 256]], 1, 0, allow_small_or_imprecise_dtypes=True), [], ["ii"])
+    V(lambda v: v.memset(T.ones[:], 1.0), [], ["ones"])
+    op("g", lambda q: q.affine_select(T.et[:], T.ones[:], [[-1, 520]], A.is_equal, 0.0, 3, 4), ["ones"], ["et"])
+    V(lambda v: v.tensor_scalar(T.pi[:, 4:5], T.pi[:, 0:1], 15, None, A.bitwise_and), ["pi"], ["qi"])
+    V(lambda v: v.memset(T.cb0[:], 1.0), [], both("cb0"))
+    V(lambda v: v.tensor_copy(T.qf[:, 0:1], T.pi[:, 4:5]), ["qi"], ["qf"])
+    V(lambda v: v.memset(T.cb1[:], 1.0), [], both("cb1"))
+    V(lambda v: v.tensor_scalar(T.inv[:, 4:5], T.qf[:, 0:1], 15.0, 511.5, A.is_equal, A.mult), ["qf"], ["inv5"])
+    V(lambda v: v.tensor_copy(T.lu[:], T.lui[:]), ["lui"], ["lu"])
+    V(lambda v: v.tensor_scalar(T.inv[:, 0:1], T.inv[:, 4:5], 0.5, None, A.add), ["inv5"], ["inv"])
+    V(lambda v: v.tensor_scalar(T.cw[:], T.k16[:], T.qf[:, 0:1], None, A.add), ["k16", "qf"], ["cw"])
+    V(lambda v: v.memset(T.cb0[:, 0:512:32], 0.0), both("cb0"), both("cb0"))
+    V(lambda v: v.memset(T.cb1[:, 0:512:32], 0.0), both("cb1"), both("cb1"))
+    V(lambda v: v.tensor_scalar(T.d1[:], T.tj[:], T.qf[:, 0:1], None, A.subtract), ["tj", "qf"], ["e"])
+    V(lambda v: v.tensor_copy(T.lid[:], T.cw[:]), ["cw"], both("lid"))
+    V(lambda v: v.tensor_scalar(T.d2[:], T.d1[:], 0.0, None, A.not_equal), ["e"], ["d2"])
+    V(lambda v: v.tensor_scalar(T.idn[:], T.ii[:], 1.0 / 512, None, A.mult), ["ii"], ["idn"])
+    V(lambda v: v.tensor_copy(T.l0[:], T.nxi[:]), ["nxi"], both("l0"))
+    S(lambda s: s.activation(T.n0[:], pick("idn", "l0"), F.Copy), ["idn"] + both("l0"), ["n0"])
+    V(lambda v: v.tensor_scalar(T.ii[:], T.d1[:], 1.0, 1023.0, A.is_equal, A.mult), ["e"], ["ii"])
+    quant("qu0", "su0", "ut", "qu0", ["ut"])
+    S(lambda s: s.activation(T.su[:, 0:128], T.su0[:, 0:128].indirect(T.lu[:, 0:8]), F.Copy), ["qu0", "lu"], ["su"])
+    S(lambda s: s.activation(T.n1[:], pick("n0", "l0"), F.Copy), ["n0"] + both("l0"), ["n1"])
+    V(lambda v: v.tensor_copy(T.qu[:, 0:128].bitcast(U32), T.qu0[:, 0:128].bitcast(U32).indirect(T.lu[:, 0:8])), ["qu0", "lu"], ["qu"])
+    quant("qx0", "sx0", "x0", "qx0.a", ["x0"])
+    quant("qx0", "sx0", "x0", "qx0.b", ["x0"], 128)
+    V(lambda v: v.tensor_tensor(T.dl[:], T.ii[:], T.d2[:], A.add), ["ii", "d2"], ["dl"])
+
+    def level_scan(k):
+        V(lambda v: v.tensor_tensor_scan(T.nsc[:], T.dl[:], T["n%d" % k][:], 0.0, A.mult, A.max), ["dl", "n%d" % k], ["nsc"])
+
+    def level_list(k):
+        V(lambda v: v.tensor_scalar(T["l%d" % k][:], T.nsc[:, 15:256:16], T.inv[:, 0:1], 1.0, A.mult, A.subtract), ["nsc", "inv"], ["l%d" % k])
+
+    def hop(k):
+        out = T["n%d" % k][:]
+        S(lambda s: s.activation(out, pick("n%d" % (k - 1), "l%d" % (k - 1)), F.Copy), ["n%d" % (k - 1)] + (both("l0") if k == 1 else ["l%d" % (k - 1)]), ["n%d" % k])
+
+    def mates_pick():
+        S(lambda s: s.activation(T.fm[:], pick("n0", "lm"), F.Copy), ["n0", "lm"], ["fm"])
+
+    def up(k, halves=(0, 1)):
+        for h in halves:
+            s = [".a", ".b"][h]
+            lo, hi = 128 * h, 128 * h + 128
+            m = "m%d" % k
+            if k == 0:
+                V(lambda v: v.tensor_copy(T.m0[:, lo:hi], half("sw", "l0", h)), both("sw") + ["l0" + s], ["m0" + s])
+                continue
+            win, l, other = ("sw", "l1", "m0") if k == 1 else ("m%d" % (k - 1), "l%d" % (k - 1), "mc%d" % (k % 2))
+            V(lambda v: v.tensor_tensor(T[m][:, lo:hi], half(win, l, h), T[other][:, lo:hi], A.max),
+              both(win) + [l, other + s], [m + s])
+            if 1 <= k <= 5:
+                c = "mc%d" % ((k + 1) % 2)
+                S(lambda q: q.activation(T[c][:, lo:hi], T[m][:, lo:hi], F.Copy), [m + s], [c + s])
+
+    def unpack(b, pb, out, factor, key, lo=0, n=C):
+        S(lambda s: s.activation(T[out][:, C * b + lo:C * b + lo + n], bank(pb, n), F.Copy, scale=factor), ["ps%d" % pb], [key])
+
+    where = {}
+
+    def names(i):
+        vb = "vbz" if i in (0, 7) else "vb%d" % (i % 2)
+        return "cb%d" % (i % 2), "n6" if i == 0 else "nb%d" % (i % 2), "rb%d" % (i % 2), vb
+
+    def d_pick(h, i):
+        cb, nb, rb, vb = names(i)
+        s, lst, k = "." + "ab"[h], where[h], 6 - i if i < 7 else 0
+        lo, hi = 128 * h, 128 * h + 128
+        if i > 0:
+            S(lambda q: q.activation(T[nb][:, lo:hi], half("n%d" % k, lst, h), F.Copy), ["n%d" % k, lst + s], [nb + s])
+        lim, cmp = ("s1", A.is_gt) if i < 7 else ("s2", A.is_le)
+        if i == 0:
+            V(lambda v: v.tensor_tensor(T[cb][:, 2 * lo + 1:2 * hi:2], T.m6[:, lo:hi], T.s1[:, lo:hi], A.is_gt), ["m6" + s, "s1" + s], [cb + s])
+            return
+        V(lambda v: v.tensor_tensor(T[cb][:, 2 * lo + 1:2 * hi:2], half("m%d" % k, lst, h), T[lim][:, lo:hi], cmp), both("m%d" % k) + [lst + s, lim + s], [cb + s])
+
+    def d_move(h, i):
+        cb, nb, rb, vb = names(i)
+        s, lo, hi = "." + "ab"[h], 128 * h, 128 * h + 128
+        V(lambda v: v.tensor_tensor_scan(T[vb][:, 2 * lo + 1:2 * hi:2], T[nb][:, lo:hi], T[cb][:, 2 * lo + 1:2 * hi:2], 0.0, A.max, A.subtract),
+          [nb if i == 0 else nb + s, cb + s], [vb + s])
+
+    def d_keep(h, i):
+        cb, nb, rb, vb = names(i)
+        s, lo, hi = "." + "ab"[h], 256 * h, 256 * h + 256
+        V(lambda v: v.tensor_tensor_scan(T[rb][:, lo:hi], T[cb][:, lo:hi], T[vb][:, lo:hi], 0.0, A.mult, A.max), [cb + s, vb + s, vb + s + "0"], [rb + s])
+
+    def d_list(h, i, lp, lb):
+        cb, nb, rb, vb = names(i)
+        s, lo, hi = "." + "ab"[h], 256 * h, 256 * h + 256
+        out = lp if i == 6 else lb if i == 7 else "lw%d" % (i % 2)
+        V(lambda v: v.tensor_scalar(T[out][:, 8 * h:8 * h + 8], T[rb][:, lo + 31:hi:32], 512.0, -1.0, A.mult, A.add), [rb + s], [out + s])
+        where[h] = out
+        if i < 6:
+            nv = "vb%d" % ((i + 1) % 2)
+            S(lambda q: q.activation(T[nv][:, lo:hi:32], T[rb][:, lo + 31:hi:32], F.Copy), [rb + s], [nv + s + "0"])
+
+    for r in range(R3):
+        d = STEP[r]
+        to = cores[(rank + d) % len(cores)]
+        qx, sx = "qx%d" % r, "sx%d" % r
+        lq, ls, zp, zb, lp, lb = ["%s%d" % (n, r) for n in ("lq", "ls", "zp", "zb", "lp", "lb")]
+        eng = len(few(cores[(rank - d) % len(cores)], core))
+        lands(lq, "arq%d" % r, 2 * eng)
+        lands(zp, "arp%d" % r, eng)
+        lands(zb + ".a", "arb%d" % r, eng)
+        lands(zb + ".b", "arc%d" % r, eng)
+        send(to, T[lq][:, 0:C].bitcast(U8), T[qx][:, 0:C].bitcast(U8), "arq%d" % r, both(qx))
+        send(to, T[ls][:, 0:C], T[sx][:, 0:C], "arq%d" % r, both(qx))
+        for h in range(2):
+            s = [".a", ".b"][h]
+            lo, hi = 128 * h, 128 * h + 128
+            mm(4 * h, ("qu", "su"), 0, (qx, sx), lo, 128, ["qu", "su", qx + s])
+            S(lambda q: q.activation(T.sw[:, lo:hi], bank(4 * h, 128), F.Copy), ["ps%d" % (4 * h)], ["sw" + s])
+
+        def limit(name, mask, f, parts):
+            for h in parts:
+                lo, hi = 128 * h, 128 * h + 128
+                V(lambda v: v.tensor_tensor(T[name][:, lo:hi], bank(4 * h, 128), T[mask][:, lo:hi], f), ["ps%d" % (4 * h), mask], [name + [".a", ".b"][h]])
+        if r == 0:
+            level_scan(1)
+            V(lambda v: v.tensor_scalar(T.mka[:], T.d2[:], -2.0 * BIG, BIG, A.mult, A.add), ["d2"], ["mka"])
+            level_list(1)
+            hop(2)
+        else:
+            level_scan(2)
+            level_list(2)
+            hop(3)
+        up(0)
+        up(1)
+        if r == 0:
+            level_scan(2)
+            V(lambda v: v.tensor_scalar(T.mkf[:], T.d2[:], 2.0 * BIG, -BIG, A.mult, A.add), ["d2"], ["mkf"])
+            level_list(2)
+            hop(3)
+            V(lambda v: v.memset(T.vbz[:], -1.0), [], both("vbz") + ["vbz.a0", "vbz.b0"])
+            V(lambda v: v.tensor_copy(T.lm[:], T.mti[:]), ["mti"], ["lm"])
+            V(lambda v: v.memset(T.vb0[:], -1.0), [], both("vb0") + ["vb0.a0", "vb0.b0"])
+            V(lambda v: v.tensor_scalar(T.vbz[:, 0:512:32], T.cw[:], 1.0, 1.0 / 512, A.add, A.mult), ["cw"], ["vbz.a0", "vbz.b0"])
+        level_scan(3)
+        limit("s2", "mkf", A.max, [0])
+        up(2)
+        level_list(3)
+        hop(4)
+        limit("s2", "mkf", A.max, [1])
+        up(3)
+        level_scan(4)
+        limit("s1", "mka", A.min, [0])
+        up(4, [0])
+        level_list(4)
+        hop(5)
+        up(4, [1])
+        for b in range(4):
+            if r == 0:
+                V(lambda v: v.quantize_mx(T.qe[:, 128 * b:128 * b + 128], T.se[:, 128 * b:128 * b + 128], T.et[:, 3 - b:515 - b]), ["et"], ["qe%d" % b])
+            if b < 2:
+                mm(1 + b, ("qe", "se"), 128 * b, (qx, sx), 0, C, ["qe%d" % b] + both(qx))
+        limit("s1", "mka", A.min, [1])
+        up(5, [0])
+        level_scan(5)
+        up(5, [1])
+        if r == 0:
+            V(lambda v: v.memset(T.vb1[:], -1.0), [], both("vb1") + ["vb1.a0", "vb1.b0"])
+        level_list(5)
+        hop(6)
+        up(6)
+        where[0] = where[1] = "lid"
+        for i in range(9):
+            if i < 8:
+                d_pick(0, i)
+            if i == 0:
+                d_pick(1, 0)
+                unpack(0, 1, "fo", 1.0, "fo.0")
+                unpack(1, 2, "fo", 1.0, "fo.1")
+            if i > 0:
+                d_keep(1, i - 1)
+            if i < 8:
+                d_move(0, i)
+            if i > 0:
+                d_list(1, i - 1, lp, lb)
+            if i == 7:
+                send(to, T[zp][:], T[lp][:], "arp%d" % r, both(lp))
+                S(lambda q: q.activation(T.vb0[:, 0:512:32], T.fw[:], F.Copy), ["fw"], ["vb0.a0", "vb0.b0"])
+            if i == 8:
+                send(to, T[zb][:, 8:16], T[lb][:, 8:16], "arc%d" % r, [lb + ".b"])
+                break
+            d_keep(0, i)
+            if i > 0:
+                d_pick(1, i)
+            d_list(0, i, lp, lb)
+            if i == 7:
+                send(to, T[zb][:, 0:8], T[lb][:, 0:8], "arb%d" % r, [lb + ".a"])
+            d_move(1, i)
+            if i == 0:
+                for b in range(4):
+                    mm([6, 7, 3, 5][b], ("qe", "se"), 128 * b, (lq, ls), 0, C, ["qe%d" % b, lq])
+            if 2 <= i <= 5:
+                unpack(i - 2, [6, 7, 3, 5][i - 2], "fa", 0.5, "fa.%d" % (i - 2))
+            if i == 6:
+                mates_pick()
+            if r == 0 and i == 5:
+                V(lambda v: v.tensor_copy(T.mf[:], T.mti[:]), ["mti"], ["mf"])
+                V(lambda v: v.tensor_scalar(T.fw[:], T.nxi[:], 1.0, 1.0 / 512, A.add, A.mult), ["nxi"], ["fw"])
+            if r == 0 and i == 6:
+                V(lambda v: v.tensor_tensor(T.mmin[:], T.mf[:], T.cw[:], A.min), ["mf", "cw"], ["mmin"])
+                V(lambda v: v.tensor_tensor(T.mmax[:], T.mf[:], T.cw[:], A.max), ["mf", "cw"], ["mmax"])
+            if r == 0 and i == 7:
+                V(lambda v: v.tensor_copy(T.lmin[:], T.mmin[:]), ["mmin"], ["lmin"])
+                V(lambda v: v.tensor_copy(T.lmax[:], T.mmax[:]), ["mmax"], ["lmax"])
+        halves = [(0, ".a", 0, 128), (1, ".b", 128, 256)]
+        for h, s, lo, hi in halves:
+            for t in range(4):
+                S(lambda q: q.activation(T.zg[:, C * t + lo:C * t + hi], T.fa[:, C * t:C * t + C].indirect(T[zp][:, 8 * h:8 * h + 8]), F.Copy),
+                  ["fa.%d" % t, zp], ["zg.%d%s" % (t, s)])
+        for h, s, lo, hi in halves:
+            V(lambda v: v.tensor_copy(T.sb[:, lo:hi], half("sw", lb, h)), both("sw") + [lb + s], ["sb" + s])
+        for h, s, lo, hi in halves:
+            V(lambda v: v.tensor_tensor(T.xm[:, lo:hi], half("sb", "lmax", h), T.mkf[:, lo:hi], A.max), both("sb") + ["lmax", "mkf"], ["xm" + s])
+        for h, s, lo, hi in halves:
+            V(lambda v: v.tensor_tensor(T.cb0[:, 2 * lo + 1:2 * hi:2], half("sb", "lmin", h), T.xm[:, lo:hi], A.is_le), both("sb") + ["lmin", "xm" + s], ["cb0" + s])
+        for h, s, lo, hi in halves:
+            V(lambda v: v.tensor_tensor_scan(T.vb0[:, 2 * lo + 1:2 * hi:2], T.fm[:, lo:hi], T.cb0[:, 2 * lo + 1:2 * hi:2], 0.0, A.max, A.subtract), ["fm", "cb0" + s], ["vb0" + s])
+        for h, s, lo, hi in halves:
+            d_keep(h, 6)
+        for h, s, lo, hi in halves:
+            V(lambda v: v.tensor_scalar(T.l0[:, 8 * h:8 * h + 8], T.rb0[:, 2 * lo + 31:2 * hi:32], 512.0, -1.0, A.mult, A.add), ["rb0" + s], ["l0" + s])
+        if r < 2:
+            S(lambda q: q.activation(T.n0[:], pick("idn", "l0"), F.Copy), ["idn"] + both("l0"), ["n0"])
+            hop(1)
+            S(lambda q: q.activation(T.fw[:], T.rb0[:, 31:512:32], F.Copy), both("rb0"), ["fw"])
+        for t in (2, 3):
+            mm(4 + t, ("qe", "se"), 128 * t, (qx, sx), 0, C, ["qe%d" % t] + both(qx))
+        def z_ready(h, s, lo, hi):
+            quant("qz", "sz", "z", "qz" + s, ["z.%d%s" % (t, s) for t in range(4)], lo)
+            for k in range(4):
+                pb = [0, 1, 2, 3, 4, 5, 0, 1][k + 4 * h]
+                mm(pb, ("wq", "wp"), 128 * k, ("qz", "sz"), lo, 128, ["wq", "wp", "qz" + s])
+                unpack(k, pb, "hh", 0.03125, "hh.%d%s" % (k, s), lo, 128)
+
+        for h, s, lo, hi in halves:
+            for t in range(4):
+                V(lambda v: v.tensor_tensor(T.z[:, 4 * lo + t:4 * hi:4], T.fa[:, C * t:C * t + C].indirect(T[zb][:, 8 * h:8 * h + 8]), T.zg[:, C * t + lo:C * t + hi], A.add),
+                  ["fa.%d" % t, zb + s, "zg.%d%s" % (t, s)], ["z.%d%s" % (t, s)])
+                if h == 1 and t == 0:
+                    z_ready(*halves[0])
+        z_ready(*halves[1])
+        if r < 2:
+            level_scan(1)
+            level_list(1)
+        else:
+            quant("qv", "sv", "vt", "qv", ["vt"])
+        xn = "x%d" % (r + 1)
+        def x_ready(h, s, lo, hi):
+            quant("qx%d" % (r + 1), "sx%d" % (r + 1), xn, "qx%d%s" % (r + 1, s), ["%s.%d%s" % (xn, t, s) for t in range(4)], lo)
+
+        for h, s, lo, hi in halves:
+            for t in (2, 3):
+                S(lambda q: q.activation(T.zg[:, C * t + lo:C * t + hi], T.hh[:, C * t:C * t + C].indirect(T[lb][:, 8 * h:8 * h + 8]), F.Copy),
+                  both("hh.%d" % t) + [lb + s], ["zg.%d%s" % (t, s)])
+        if r < 2:
+            hop(2)
+        for h, s, lo, hi in halves:
+            for t in (0, 1):
+                V(lambda v: v.tensor_tensor(T[xn][:, 4 * lo + t:4 * hi:4], T.hh[:, C * t:C * t + C].indirect(T[lb][:, 8 * h:8 * h + 8]), T.fo[:, C * t + lo:C * t + hi], A.add),
+                  both("hh.%d" % t) + ["fo.%d" % t, lb + s], ["%s.%d%s" % (xn, t, s)])
+        for h, s, lo, hi in halves:
+            for t in (2, 3):
+                V(lambda v: v.tensor_tensor(T[xn][:, 4 * lo + t:4 * hi:4], T.zg[:, C * t + lo:C * t + hi], T.ps[:, 512 * (4 + t) + lo:512 * (4 + t) + hi], A.add),
+                  ["zg.%d%s" % (t, s), "ps%d" % (4 + t)], ["%s.%d%s" % (xn, t, s)])
+                if h == 1 and t == 2:
+                    x_ready(*halves[0])
+        x_ready(*halves[1])
+        if r == 2:
+            S(lambda q: q.activation(T.nff[:], pick("idn", "l0"), F.Identity, bias=-1.0, scale=512.0), ["idn"] + both("l0"), ["nff"])
+    op("y", lambda q: q.dma_start(T.nf[:], T.nff[0:128:16, :]), ["nff"], [], "dnf", 16)
+    op("y", lambda q: q.dma_start(T.oc[:], T.qx3[:, 0:C].bitcast(U8)), both("qx3"), [], "doc", 16)
+    for h in range(2):
+        mm(6 + h, ("qv", "sv"), 0, ("qx3", "sx3"), 128 * h, 128, ["qv", "qx3" + [".a", ".b"][h]])
+    V(lambda v: v.tensor_copy(T.yt[:, 0:128], bank(6, 128)), ["ps6"], ["yt.0"])
+    for k in range(2):
+        op("s", lambda q: q.dma_start(T.osc[4 * k:4 * k + 4, 0:C], T.sx3[32 * k:32 * k + 4, 0:C]), both("qx3"), [], "dos%d" % k, 16)
+    S(lambda s: s.activation(T.yt[:, 128:256], bank(7, 128), F.Copy), ["ps7"], ["yt.1"])
+    op("y", lambda q: q.dma_start(T.y[:, 0:128], T.yt[:, 0:128]), ["yt.0"], [], "dy0", 16)
+    op("s", lambda q: q.dma_start(T.y[:, 128:256], T.yt[:, 128:256]), ["yt.1"], [], "dy1", 16)
+    for k in range(2, 4):
+        op("y", lambda q: q.dma_start(T.osc[4 * k:4 * k + 4, 0:C], T.sx3[32 * k:32 * k + 4, 0:C]), both("qx3"), [], "dos%d" % k, 16)
+    for s, n in count.items():
+        g.wait_ge(T.sem[s], n)
+    g.wait_ge(T.sem.sent, sent[0])

@@ -4,60 +4,24 @@ STEP = [1, 2, 4]
 C = 256
 R3 = 3
 CODE = "float8_e4m3fn_x4"
-SCRATCH = {
-    "ps": ("psum", [128, 4096], "float32"),
-    "ut": ("sbuf", [128, 512], "bfloat16"), "vt": ("sbuf", [128, 512], "bfloat16"),
-    "qu0": ("sbuf", [128, 128], CODE), "su0": ("sbuf", [128, 128], "uint8"),
-    "qu": ("sbuf", [128, 128], CODE), "su": ("sbuf", [128, 128], "uint8"),
-    "qv": ("sbuf", [128, 128], CODE), "sv": ("sbuf", [128, 128], "uint8"),
-    "wq": ("sbuf", [128, 512], CODE), "wp": ("sbuf", [128, 512], "uint8"),
-    "ones": ("sbuf", [128, 520], "bfloat16"), "et": ("sbuf", [128, 520], "bfloat16"),
-    "qe": ("sbuf", [128, 512], CODE), "se": ("sbuf", [128, 512], "uint8"),
-    "nxi": ("sbuf", [128, 16], "int32"), "mti": ("sbuf", [128, 16], "int32"),
-    "tj": ("sbuf", [128, 256], "float32"), "ii": ("sbuf", [128, 256], "float32"),
-    "idn": ("sbuf", [128, 256], "bfloat16"),
-    "pi": ("sbuf", [128, 8], "int32"), "qf": ("sbuf", [128, 8], "float32"), "inv": ("sbuf", [128, 8], "float32"),
-    "k16": ("sbuf", [128, 16], "float32"), "cw": ("sbuf", [128, 16], "float32"),
-    "d1": ("sbuf", [128, 256], "float32"), "d2": ("sbuf", [128, 256], "float32"),
-    "mka": ("sbuf", [128, 256], "float32"),
-    "mkf": ("sbuf", [128, 256], "float32"),
-    "dl": ("sbuf", [128, 256], "bfloat16"),
-    "lid": ("sbuf", [128, 16], "uint16"), "lu": ("sbuf", [128, 8], "uint16"), "lui": ("sbuf", [128, 8], "int32"),
-    "lm": ("sbuf", [128, 16], "uint16"), "lmin": ("sbuf", [128, 16], "uint16"), "lmax": ("sbuf", [128, 16], "uint16"),
-    "mf": ("sbuf", [128, 16], "float32"), "mmin": ("sbuf", [128, 16], "float32"), "mmax": ("sbuf", [128, 16], "float32"),
-    "sw": ("sbuf", [128, 256], "float32"), "s1": ("sbuf", [128, 256], "float32"), "s2": ("sbuf", [128, 256], "float32"),
-    "n6": ("sbuf", [128, 256], "bfloat16"), "nsc": ("sbuf", [128, 256], "bfloat16"),
-    "fm": ("sbuf", [128, 256], "bfloat16"), "fw": ("sbuf", [128, 16], "bfloat16"),
-    "sb": ("sbuf", [128, 256], "float32"), "xm": ("sbuf", [128, 256], "float32"),
-    "nff": ("sbuf", [128, 256], "float32"), "yt": ("sbuf", [128, 256], "float32"),
-    "fa": ("sbuf", [128, 1024], "bfloat16"), "fo": ("sbuf", [128, 1024], "bfloat16"),
-    "zg": ("sbuf", [128, 1024], "bfloat16"), "z": ("sbuf", [128, 1024], "bfloat16"), "hh": ("sbuf", [128, 1024], "bfloat16"),
-    "qz": ("sbuf", [128, 256], CODE), "sz": ("sbuf", [128, 256], "uint8"),
-    "vbz": ("sbuf", [128, 512], "bfloat16"),
-}
-for _i in range(2):
-    SCRATCH["mc%d" % _i] = ("sbuf", [128, 256], "float32")
-    for _n in ("cb", "vb", "rb"):
-        SCRATCH["%s%d" % (_n, _i)] = ("sbuf", [128, 512], "bfloat16")
-    SCRATCH["nb%d" % _i] = ("sbuf", [128, 256], "bfloat16")
-    SCRATCH["lw%d" % _i] = ("sbuf", [128, 16], "uint16")
-for _i in range(4):
-    SCRATCH["x%d" % _i] = ("sbuf", [128, 1024], "bfloat16")
-    SCRATCH["qx%d" % _i] = ("sbuf", [128, 256], CODE)
-    SCRATCH["sx%d" % _i] = ("sbuf", [128, 256], "uint8")
-for _i in range(3):
-    SCRATCH["lq%d" % _i] = ("sbuf", [128, 256], CODE)
-    SCRATCH["ls%d" % _i] = ("sbuf", [128, 256], "uint8")
-    for _n in ("lp", "lb", "zp", "zb"):
-        SCRATCH["%s%d" % (_n, _i)] = ("sbuf", [128, 16], "uint16")
-for _i in range(7):
-    SCRATCH["m%d" % _i] = ("sbuf", [128, 256], "float32")
-for _i in range(6):
-    SCRATCH["n%d" % _i] = ("sbuf", [128, 256], "bfloat16")
-    SCRATCH["l%d" % _i] = ("sbuf", [128, 16], "uint16")
-DMAS = ["dx", "dnx", "dmt", "du", "dwc", "dws", "dv", "doc", "dos0", "dos1", "dos2", "dos3", "dy0", "dy1", "dnf"]
-SEMAPHORES = ["cv", "cs", "ct", "cg", "sent"] + DMAS + ["%s%d" % (n, i) for n in ("arq", "arp", "arb", "arc") for i in range(3)]
+UNIT = 2.0 ** 71
 BIG = 1.0e29
+KEY = 1024.0 * UNIT
+LISTS = "l0 l1 l2 l3 l4 l5 l6 lp0 lp1 lp2 lb0 lb1 lb2".split()
+SCRATCH = {"ps": ("psum", [128, 4096], "float32")}
+for _names, _cols, _type in [
+        ("ut vt", 512, "bfloat16"), ("qu0 qu qp qv", 128, CODE), ("su0 su sp sv", 128, "uint8"), ("wq qe", 512, CODE), ("wp se", 512, "uint8"),
+        ("ones et", 520, "bfloat16"), ("nxi mti pi ti", 16, "int32"), ("e5 col bias kk cw dm df thr sm", 16, "float32"), ("ex exd exo", 32, "float32"),
+        ("tj ii d1 idm cwin wn wa a0 a1 a2 b0 b1 b2 b3 yy s1 s2 yn yp sg yt", 256, "float32"), ("sw", 512, "float32"), ("tw", 304, "float32"), ("fw1", 544, "float32"),
+        ("idn dl nsa nsb n3t abf od ev fl xr rt rb rp xf xs", 256, "bfloat16"), ("ta", 304, "bfloat16"), ("fw2 xt", 544, "bfloat16"), ("nf2 rc", 512, "bfloat16"), ("zt", 272, "bfloat16"),
+        ("cz ch", 32, "bfloat16"), ("lu lv lm lc l2s lq2 lsg", 16, "uint16"), ("ll", 16 * len(LISTS), "uint16"),
+        ("fa fo zg z hh x0 x1 x2 x3", 1024, "bfloat16"), ("qz qx0 qx1 qx2 qx3 lq0 lq1 lq2c", 256, CODE), ("sz sx0 sx1 sx2 sx3 ls0 ls1 ls2", 256, "uint8"),
+        ("zp0 zp1 zp2 zb0 zb1 zb2", 16, "uint16"),
+        ("f0 f1 n1 n2 n3 n4 n5 n6 n7", 256, "bfloat16")]:
+    for _n in _names.split():
+        SCRATCH[_n] = ("sbuf", [128, _cols], _type)
+DMAS = ["dx", "dnx", "dmt", "du", "dwc", "dws", "dv", "doc", "dos0", "dos1", "dos2", "dos3", "dy0", "dy1", "dnf"]
+SEMAPHORES = ["cv", "cs", "ct", "cg", "sent"] + DMAS + ["%s%d" % (n, i) for n in ("arq", "arp", "arb") for i in range(3)]
 
 
 def make_issue(g, T):
@@ -124,6 +88,7 @@ def rank_program(g, core, T, topo):
     cores = T.cores
     U8, U32 = dt.uint8, dt.uint32
     sent = [0]
+    halves = [(0, ".a", 0, 128), (1, ".b", 128, 256)]
 
     def few(src, dst):
         return topo.engines(src, dst)[:8]
@@ -141,6 +106,9 @@ def rank_program(g, core, T, topo):
     def S(call, reads, writes):
         op("s", call, reads, writes)
 
+    def G(call, reads, writes):
+        op("g", call, reads, writes)
+
     def both(name):
         return [name + ".a", name + ".b"]
 
@@ -155,11 +123,17 @@ def rank_program(g, core, T, topo):
     def quant(q, s, tile, key, reads, lo=0, n=128):
         V(lambda v: v.quantize_mx(T[q][:, lo:lo + n], T[s][:, lo:lo + n], T[tile][:, 4 * lo:4 * lo + 4 * n]), reads, [key])
 
-    def pick(win, lst, a=0):
-        return T[win][:, a:a + C].indirect(T[lst][:, 0:16])
+    def L(lst, a=0, b=16):
+        if lst in LISTS:
+            return T.ll[:, 16 * LISTS.index(lst) + a:16 * LISTS.index(lst) + b]
+        return T[lst][:, a:b]
 
-    def half(win, lst, h):
-        return T[win][:, 0:C].indirect(T[lst][:, 8 * h:8 * h + 8])
+    def pick(win, lst, n=C):
+        return T[win][:, 0:n].indirect(L(lst))
+
+    def col(k):
+        return T.col[:, k:k + 1]
+    STEPS, KEYS, NOKEY, EDGE, INV, OFF0, OFF1, LOW, LANE, SLOT = range(10)
 
     op("y", lambda q: q.dma_start(T.nxi[:], T.nx[:]), [], ["nxi"], "dnx", 16)
     op("s", lambda q: q.dma_start(T.x0[:], T.x[:]), [], ["x0"], "dx", 16)
@@ -169,243 +143,253 @@ def rank_program(g, core, T, topo):
     op("y", lambda q: q.dma_start(T.wp[:, 0:512], T.ws[:]), [], ["wp"], "dws", 16)
     op("y", lambda q: q.dma_start(T.vt[:], T.v[:]), [], ["vt"], "dv", 16)
 
-    op("g", lambda q: q.iota(T.pi[:, 0:1], [[0, 1]], 0, 1), [], ["pi"])
-    op("g", lambda q: q.iota(T.lui[:], [[16, 8]], 0, 0), [], ["lui"])
-    op("g", lambda q: q.iota(T.k16[:], [[16, 16]], 0, 0, allow_small_or_imprecise_dtypes=True), [], ["k16"])
-    op("g", lambda q: q.iota(T.tj[:], [[0, 16], [1, 16]], 0, 0, allow_small_or_imprecise_dtypes=True), [], ["tj"])
-    op("g", lambda q: q.iota(T.ii[:], [[1, 256]], 1, 0, allow_small_or_imprecise_dtypes=True), [], ["ii"])
+    G(lambda q: q.iota(T.pi[:, 0:1], [[0, 1]], 0, 1), [], ["pi"])
+    G(lambda q: q.iota(T.ii[:], [[1, 256]], 1, 0, allow_small_or_imprecise_dtypes=True), [], ["ii"])
+    G(lambda q: q.iota(T.cw[:], [[16, 16]], 0, 0, allow_small_or_imprecise_dtypes=True), [], ["k16"])
+    G(lambda q: q.iota(T.tj[:], [[0, 16], [1, 16]], 0, 0, allow_small_or_imprecise_dtypes=True), [], ["tj"])
     V(lambda v: v.memset(T.ones[:], 1.0), [], ["ones"])
-    op("g", lambda q: q.affine_select(T.et[:], T.ones[:], [[-1, 520]], A.is_equal, 0.0, 3, 4), ["ones"], ["et"])
-    V(lambda v: v.tensor_scalar(T.pi[:, 4:5], T.pi[:, 0:1], 15, None, A.bitwise_and), ["pi"], ["qi"])
-    V(lambda v: v.memset(T.cb0[:], 1.0), [], both("cb0"))
-    V(lambda v: v.tensor_copy(T.qf[:, 0:1], T.pi[:, 4:5]), ["qi"], ["qf"])
-    V(lambda v: v.memset(T.cb1[:], 1.0), [], both("cb1"))
-    V(lambda v: v.tensor_scalar(T.inv[:, 4:5], T.qf[:, 0:1], 15.0, 511.5, A.is_equal, A.mult), ["qf"], ["inv5"])
-    V(lambda v: v.tensor_copy(T.lu[:], T.lui[:]), ["lui"], ["lu"])
-    V(lambda v: v.tensor_scalar(T.inv[:, 0:1], T.inv[:, 4:5], 0.5, None, A.add), ["inv5"], ["inv"])
-    V(lambda v: v.tensor_scalar(T.cw[:], T.k16[:], T.qf[:, 0:1], None, A.add), ["k16", "qf"], ["cw"])
-    V(lambda v: v.memset(T.cb0[:, 0:512:32], 0.0), both("cb0"), both("cb0"))
-    V(lambda v: v.memset(T.cb1[:, 0:512:32], 0.0), both("cb1"), both("cb1"))
-    V(lambda v: v.tensor_scalar(T.d1[:], T.tj[:], T.qf[:, 0:1], None, A.subtract), ["tj", "qf"], ["e"])
-    V(lambda v: v.tensor_copy(T.lid[:], T.cw[:]), ["cw"], both("lid"))
-    V(lambda v: v.tensor_scalar(T.d2[:], T.d1[:], 0.0, None, A.not_equal), ["e"], ["d2"])
-    V(lambda v: v.tensor_scalar(T.idn[:], T.ii[:], 1.0 / 512, None, A.mult), ["ii"], ["idn"])
-    V(lambda v: v.tensor_copy(T.l0[:], T.nxi[:]), ["nxi"], both("l0"))
-    S(lambda s: s.activation(T.n0[:], pick("idn", "l0"), F.Copy), ["idn"] + both("l0"), ["n0"])
-    V(lambda v: v.tensor_scalar(T.ii[:], T.d1[:], 1.0, 1023.0, A.is_equal, A.mult), ["e"], ["ii"])
+    G(lambda q: q.affine_select(T.et[:], T.ones[:], [[-1, 520]], A.is_equal, 0.0, 3, 4), ["ones"], ["et"])
+    for k, m in enumerate((1, 2, 4, 8, 16, 15, 7, 31)):
+        V(lambda v: v.tensor_scalar(T.ti[:, k:k + 1], T.pi[:, 0:1], m, None, A.bitwise_and), ["pi"], ["ti%d" % k])
+    for k in range(3):
+        V(lambda v: v.memset(T.kk[:, k:k + 1], KEY * 2 ** k), [], ["kk%d" % k])
+    ti = ["ti%d" % k for k in range(8)]
+    V(lambda v: v.tensor_scalar(T.e5[:, 0:5], T.ti[:, 0:5], 0.0, None, A.is_equal), ti, ["e5"])
+    V(lambda v: v.tensor_copy(T.e5[:, 5:8], T.ti[:, 5:8]), ti, ["e8"])
+    score, even, lane = T.e5[:, 3:4], T.e5[:, 4:5], T.e5[:, 5:6]
+    V(lambda v: v.tensor_scalar(T.lu[:, 0:8], T.cw[:, 0:8], 0.0, None, A.add), ["k16"], ["lu"])
+    V(lambda v: v.tensor_scalar(T.idn[:], T.ii[:], UNIT, None, A.mult), ["ii"], ["idn"])
+    V(lambda v: v.tensor_scalar(col(STEPS), score, -UNIT, UNIT, A.mult, A.add), ["e5"], ["c0"])
+    V(lambda v: v.tensor_scalar(col(LOW), score, -BIG, None, A.mult), ["e5"], ["c7"])
+    V(lambda v: v.tensor_scalar(T.sm[:, 0:1], lane, 15.0, None, A.is_equal), ["e8"], ["sm0"])
+    V(lambda v: v.tensor_scalar(T.d1[:], T.tj[:], lane, None, A.subtract), ["tj", "e8"], ["d1"])
+    V(lambda v: v.tensor_copy(L("l0"), T.nxi[:]), ["nxi"], ["l0"])
+    S(lambda s: s.activation(T.f0[:], pick("idn", "l0"), F.Copy), ["idn", "l0"], ["f0"])
+    V(lambda v: v.tensor_scalar(T.tj[:], T.d1[:], 1.0, 1023.0, A.is_equal, A.mult), ["d1"], ["tj"])
+    V(lambda v: v.tensor_scalar(col(INV), T.sm[:, 0:1], 1023.0 / 1024 / UNIT, 1.0 / 1024 / UNIT, A.mult, A.add), ["sm0"], ["c4"])
+    V(lambda v: v.tensor_scalar(T.d1[:], T.d1[:], 0.0, None, A.not_equal), ["d1"], ["d1"])
     quant("qu0", "su0", "ut", "qu0", ["ut"])
-    S(lambda s: s.activation(T.su[:, 0:128], T.su0[:, 0:128].indirect(T.lu[:, 0:8]), F.Copy), ["qu0", "lu"], ["su"])
-    S(lambda s: s.activation(T.n1[:], pick("n0", "l0"), F.Copy), ["n0"] + both("l0"), ["n1"])
+    V(lambda v: v.tensor_tensor(T.dl[:], T.tj[:], T.d1[:], A.add), ["tj", "d1"], ["dl"])
+    S(lambda s: s.activation(T.n1[:], pick("f0", "l0"), F.Copy), ["f0", "l0"], ["n1"])
     V(lambda v: v.tensor_copy(T.qu[:, 0:128].bitcast(U32), T.qu0[:, 0:128].bitcast(U32).indirect(T.lu[:, 0:8])), ["qu0", "lu"], ["qu"])
+    S(lambda s: s.activation(T.su[:, 0:128], T.su0[:, 0:128].indirect(T.lu[:, 0:8]), F.Copy), ["qu0", "lu"], ["su"])
     quant("qx0", "sx0", "x0", "qx0.a", ["x0"])
     quant("qx0", "sx0", "x0", "qx0.b", ["x0"], 128)
-    V(lambda v: v.tensor_tensor(T.dl[:], T.ii[:], T.d2[:], A.add), ["ii", "d2"], ["dl"])
+    S(lambda s: s.activation(T.idm[:], T.ii[:], F.Identity, scale=col(STEPS)), ["ii", "c0"], ["idm"])
+    S(lambda s: s.activation(T.cwin[:], T.ii[:], F.Identity, scale=col(STEPS), bias=col(LOW)), ["ii", "c0", "c7"], ["cwin"])
 
-    def level_scan(k):
-        V(lambda v: v.tensor_tensor_scan(T.nsc[:], T.dl[:], T["n%d" % k][:], 0.0, A.mult, A.max), ["dl", "n%d" % k], ["nsc"])
+    def more_constants(part):
+        if part == 0:
+            V(lambda v: v.tensor_scalar(T.bias[:, 0:3], T.e5[:, 0:3], BIG, -BIG, A.mult, A.add), ["e5"], ["bias0"])
+            V(lambda v: v.tensor_scalar(T.kk[:, 4:7], T.kk[:, 0:3], 1.0 / UNIT, col(STEPS), A.mult, A.mult), ["kk0", "kk1", "kk2", "c0"], ["kk"])
+            V(lambda v: v.tensor_scalar(T.sm[:, 1:2], T.e5[:, 6:7], -1024.0, 7168.0, A.mult, A.add), ["e8"], ["sm1"])
+            V(lambda v: v.tensor_tensor(T.bias[:, 4:7], T.bias[:, 0:3], T.kk[:, 4:7], A.add), ["bias0", "kk"], ["bias"])
+            V(lambda v: v.tensor_tensor(col(KEYS), T.sm[:, 1:2], col(STEPS), A.mult), ["sm1", "c0"], ["c1"])
+        if part == 1:
+            V(lambda v: v.tensor_scalar(T.lv[:, 0:8:2], T.cw[:, 0:8:2], 16.0, None, A.add), ["k16"], ["lv0"])
+            V(lambda v: v.tensor_scalar(T.lv[:, 1:8:2], T.cw[:, 1:8:2], -16.0, None, A.add), ["k16"], ["lv1"])
+            V(lambda v: v.tensor_scalar(col(NOKEY), col(KEYS), -1.0, None, A.mult), ["c1"], ["c2"])
+            V(lambda v: v.tensor_scalar(T.sm[:, 2:3], T.e5[:, 7:8], 1.0, None, A.add), ["e8"], ["sm2"])
+            V(lambda v: v.memset(T.cz[:, 0:1], UNIT), [], ["cz0"])
+            V(lambda v: v.tensor_copy(T.qp[:, 0:128].bitcast(U32), T.qu0[:, 0:128].bitcast(U32).indirect(T.lv[:, 0:8])), ["qu0", "lv0", "lv1"], ["qp"])
+            S(lambda s: s.activation(T.sp[:, 0:128], T.su0[:, 0:128].indirect(T.lv[:, 0:8]), F.Copy), ["qu0", "lv0", "lv1"], ["sp"])
+            for e in range(2):
+                V(lambda v: v.tensor_scalar(T.cz[:, 1 + e:17:2], T.cw[:, 0:16:2], T.sm[:, 2:3], UNIT, A.add, A.mult), ["k16", "sm2"], ["cz%d" % (1 + e)])
+        if part == 2:
+            V(lambda v: v.tensor_scalar(T.sm[:, 3:4], score, 15.0 / 16, 1.0 / 16, A.mult, A.add), ["e5"], ["sm3"])
+            V(lambda v: v.tensor_scalar(T.sm[:, 4:5], score, -272.0, 288.0, A.mult, A.add), ["e5"], ["sm4"])
+            V(lambda v: v.memset(T.tw[:, 0:16], 0.0), [], ["tw0"])
+            V(lambda v: v.memset(T.tw[:, 272:288], 0.0), [], ["tw1"])
+            V(lambda v: v.tensor_scalar(T.lc[:], T.cw[:], T.sm[:, 3:4], T.sm[:, 4:5], A.mult, A.add), ["k16", "sm3", "sm4"], ["lc"])
+            V(lambda v: v.memset(T.ta[:, 0:16], 0.0), [], ["ta0"])
+            V(lambda v: v.memset(T.ta[:, 272:304], 0.0), [], ["tac"])
+            V(lambda v: v.memset(T.zt[:, 0:16], 0.0), [], ["zt0"])
+        if part == 3:
+            V(lambda v: v.tensor_scalar(col(OFF0), even, -256.0, 255.0, A.mult, A.add), ["e5"], ["c5"])
+            V(lambda v: v.tensor_scalar(col(OFF1), even, 288.0, -1.0, A.mult, A.add), ["e5"], ["c6"])
+            V(lambda v: v.tensor_scalar(T.sm[:, 5:6], even, -272.0, 272.0, A.mult, A.add), ["e5"], ["sm5"])
+            V(lambda v: v.tensor_scalar(T.sm[:, 6:7], even, 240.0, None, A.mult), ["e5"], ["sm6"])
+            V(lambda v: v.tensor_scalar(T.sm[:, 7:8], T.sm[:, 0:1], -2.0 * BIG, BIG, A.mult, A.add), ["sm0"], ["sm7"])
+            for e in range(2):
+                V(lambda v: v.tensor_scalar(T.l2s[:, e:16:2], T.cw[:, e:16:2], T.sm[:, 5 + e:6 + e], lane, A.add, A.add), ["k16", "sm5", "sm6", "e8"], ["l2s%d" % e])
+            V(lambda v: v.tensor_scalar(col(EDGE), T.sm[:, 7:8], 1.0 / UNIT, col(STEPS), A.mult, A.mult), ["sm7", "c0"], ["c3"])
+            V(lambda v: v.tensor_scalar(T.exd[:, 1:32:2], T.cw[:], lane, None, A.add), ["k16", "e8"], ["exd1"])
+            V(lambda v: v.tensor_scalar(T.ch[:, 0:16], T.exd[:, 1:32:2], 1.0, UNIT, A.add, A.mult), ["exd1"], ["ch"])
+        if part == 4:
+            V(lambda v: v.tensor_copy(T.lm[:], T.mti[:]), ["mti"], ["lm"])
+            V(lambda v: v.tensor_tensor(T.exd[:, 0:32:2], T.mti[:], T.exd[:, 1:32:2], A.subtract), ["mti", "exd1"], ["exd0"])
+            V(lambda v: v.memset(T.ex[:, 0:32:2], 0.0), [], ["ex0"])
+            V(lambda v: v.tensor_scalar(T.thr[:, 0:1], T.sm[:, 0:1], -511.5, 512.0, A.mult, A.add), ["sm0"], ["thr"])
+            V(lambda v: v.tensor_tensor(T.yy[:], pick("ii", "lm"), T.tj[:], A.is_gt), ["ii", "lm", "tj2"], ["yy"])
+        if part == 5:
+            V(lambda v: v.tensor_scalar(T.sg[:], T.yy[:], 2.0, -1.0, A.mult, A.add), ["yy"], ["sg"])
 
-    def level_list(k):
-        V(lambda v: v.tensor_scalar(T["l%d" % k][:], T.nsc[:, 15:256:16], T.inv[:, 0:1], 1.0, A.mult, A.subtract), ["nsc", "inv"], ["l%d" % k])
+    flip = [0]
 
-    def hop(k):
-        out = T["n%d" % k][:]
-        S(lambda s: s.activation(out, pick("n%d" % (k - 1), "l%d" % (k - 1)), F.Copy), ["n%d" % (k - 1)] + (both("l0") if k == 1 else ["l%d" % (k - 1)]), ["n%d" % k])
+    def n_name(r, k):
+        return "f%d" % (r % 2) if k == 0 else "n%d" % k
 
-    def mates_pick():
-        S(lambda s: s.activation(T.fm[:], pick("n0", "lm"), F.Copy), ["n0", "lm"], ["fm"])
+    def level_scan(r, k):
+        flip[0] ^= 1
+        o, n = ["nsa", "nsb"][flip[0]], n_name(r, k)
+        V(lambda v: v.tensor_tensor_scan(T[o][:], T.dl[:], T[n][:], 0.0, A.mult, A.max), ["dl", n], [o])
+        return o
 
-    def up(k, halves=(0, 1)):
-        for h in halves:
-            s = [".a", ".b"][h]
-            lo, hi = 128 * h, 128 * h + 128
-            m = "m%d" % k
-            if k == 0:
-                V(lambda v: v.tensor_copy(T.m0[:, lo:hi], half("sw", "l0", h)), both("sw") + ["l0" + s], ["m0" + s])
-                continue
-            win, l, other = ("sw", "l1", "m0") if k == 1 else ("m%d" % (k - 1), "l%d" % (k - 1), "mc%d" % (k % 2))
-            V(lambda v: v.tensor_tensor(T[m][:, lo:hi], half(win, l, h), T[other][:, lo:hi], A.max),
-              both(win) + [l, other + s], [m + s])
-            if 1 <= k <= 5:
-                c = "mc%d" % ((k + 1) % 2)
-                S(lambda q: q.activation(T[c][:, lo:hi], T[m][:, lo:hi], F.Copy), [m + s], [c + s])
+    def level_list(o, k):
+        V(lambda v: v.tensor_scalar(L("l%d" % k), T[o][:, 15:256:16], col(INV), 1.0, A.mult, A.subtract), [o, "c4"], ["l%d" % k])
+
+    def hop(r, k):
+        n = n_name(r, k - 1)
+        S(lambda s: s.activation(T["n%d" % k][:], pick(n, "l%d" % (k - 1)), F.Copy), [n, "l%d" % (k - 1)], ["n%d" % k])
+
+    def window(src, k):
+        b = T.bias[:, 4 + k:5 + k]
+        S(lambda s: s.activation(T.wa[:, 0:128], T[src][:, 0:128], F.Identity, bias=b), [src, "bias"], ["wa.a"])
+        V(lambda v: v.tensor_scalar(T.wa[:, 128:256], T[src][:, 128:256], b, None, A.add), [src, "bias"], ["wa.b"])
+
+    def grow(out, src, lst):
+        V(lambda v: v.tensor_tensor(T[out][:, 0:C], pick("wa", lst), T[src][:, 0:C], A.max), both("wa") + [lst, src], [out])
+
+    def turn(out, src, reads, writes):
+        V(lambda v: v.transpose(out, src), reads, writes)
 
     def unpack(b, pb, out, factor, key, lo=0, n=C):
         S(lambda s: s.activation(T[out][:, C * b + lo:C * b + lo + n], bank(pb, n), F.Copy, scale=factor), ["ps%d" % pb], [key])
 
-    where = {}
-
-    def names(i):
-        vb = "vbz" if i in (0, 7) else "vb%d" % (i % 2)
-        return "cb%d" % (i % 2), "n6" if i == 0 else "nb%d" % (i % 2), "rb%d" % (i % 2), vb
-
-    def d_pick(h, i):
-        cb, nb, rb, vb = names(i)
-        s, lst, k = "." + "ab"[h], where[h], 6 - i if i < 7 else 0
-        lo, hi = 128 * h, 128 * h + 128
-        if i > 0:
-            S(lambda q: q.activation(T[nb][:, lo:hi], half("n%d" % k, lst, h), F.Copy), ["n%d" % k, lst + s], [nb + s])
-        lim, cmp = ("s1", A.is_gt) if i < 7 else ("s2", A.is_le)
-        if i == 0:
-            V(lambda v: v.tensor_tensor(T[cb][:, 2 * lo + 1:2 * hi:2], T.m6[:, lo:hi], T.s1[:, lo:hi], A.is_gt), ["m6" + s, "s1" + s], [cb + s])
-            return
-        V(lambda v: v.tensor_tensor(T[cb][:, 2 * lo + 1:2 * hi:2], half("m%d" % k, lst, h), T[lim][:, lo:hi], cmp), both("m%d" % k) + [lst + s, lim + s], [cb + s])
-
-    def d_move(h, i):
-        cb, nb, rb, vb = names(i)
-        s, lo, hi = "." + "ab"[h], 128 * h, 128 * h + 128
-        V(lambda v: v.tensor_tensor_scan(T[vb][:, 2 * lo + 1:2 * hi:2], T[nb][:, lo:hi], T[cb][:, 2 * lo + 1:2 * hi:2], 0.0, A.max, A.subtract),
-          [nb if i == 0 else nb + s, cb + s], [vb + s])
-
-    def d_keep(h, i):
-        cb, nb, rb, vb = names(i)
-        s, lo, hi = "." + "ab"[h], 256 * h, 256 * h + 256
-        V(lambda v: v.tensor_tensor_scan(T[rb][:, lo:hi], T[cb][:, lo:hi], T[vb][:, lo:hi], 0.0, A.mult, A.max), [cb + s, vb + s, vb + s + "0"], [rb + s])
-
-    def d_list(h, i, lp, lb):
-        cb, nb, rb, vb = names(i)
-        s, lo, hi = "." + "ab"[h], 256 * h, 256 * h + 256
-        out = lp if i == 6 else lb if i == 7 else "lw%d" % (i % 2)
-        V(lambda v: v.tensor_scalar(T[out][:, 8 * h:8 * h + 8], T[rb][:, lo + 31:hi:32], 512.0, -1.0, A.mult, A.add), [rb + s], [out + s])
-        where[h] = out
-        if i < 6:
-            nv = "vb%d" % ((i + 1) % 2)
-            S(lambda q: q.activation(T[nv][:, lo:hi:32], T[rb][:, lo + 31:hi:32], F.Copy), [rb + s], [nv + s + "0"])
-
     for r in range(R3):
         d = STEP[r]
+        first = r == 0
         to = cores[(rank + d) % len(cores)]
         qx, sx = "qx%d" % r, "sx%d" % r
-        lq, ls, zp, zb, lp, lb = ["%s%d" % (n, r) for n in ("lq", "ls", "zp", "zb", "lp", "lb")]
+        ls, zp, zb, lp, lb = ["%s%d" % (n, r) for n in ("ls", "zp", "zb", "lp", "lb")]
+        lq = ["lq0", "lq1", "lq2c"][r]
         eng = len(few(cores[(rank - d) % len(cores)], core))
         lands(lq, "arq%d" % r, 2 * eng)
         lands(zp, "arp%d" % r, eng)
-        lands(zb + ".a", "arb%d" % r, eng)
-        lands(zb + ".b", "arc%d" % r, eng)
+        lands(zb, "arb%d" % r, eng)
         send(to, T[lq][:, 0:C].bitcast(U8), T[qx][:, 0:C].bitcast(U8), "arq%d" % r, both(qx))
         send(to, T[ls][:, 0:C], T[sx][:, 0:C], "arq%d" % r, both(qx))
-        for h in range(2):
-            s = [".a", ".b"][h]
-            lo, hi = 128 * h, 128 * h + 128
-            mm(4 * h, ("qu", "su"), 0, (qx, sx), lo, 128, ["qu", "su", qx + s])
-            S(lambda q: q.activation(T.sw[:, lo:hi], bank(4 * h, 128), F.Copy), ["ps%d" % (4 * h)], ["sw" + s])
-
-        def limit(name, mask, f, parts):
-            for h in parts:
-                lo, hi = 128 * h, 128 * h + 128
-                V(lambda v: v.tensor_tensor(T[name][:, lo:hi], bank(4 * h, 128), T[mask][:, lo:hi], f), ["ps%d" % (4 * h), mask], [name + [".a", ".b"][h]])
-        if r == 0:
-            level_scan(1)
-            V(lambda v: v.tensor_scalar(T.mka[:], T.d2[:], -2.0 * BIG, BIG, A.mult, A.add), ["d2"], ["mka"])
-            level_list(1)
-            hop(2)
-        else:
-            level_scan(2)
-            level_list(2)
-            hop(3)
-        up(0)
-        up(1)
-        if r == 0:
-            level_scan(2)
-            V(lambda v: v.tensor_scalar(T.mkf[:], T.d2[:], 2.0 * BIG, -BIG, A.mult, A.add), ["d2"], ["mkf"])
-            level_list(2)
-            hop(3)
-            V(lambda v: v.memset(T.vbz[:], -1.0), [], both("vbz") + ["vbz.a0", "vbz.b0"])
-            V(lambda v: v.tensor_copy(T.lm[:], T.mti[:]), ["mti"], ["lm"])
-            V(lambda v: v.memset(T.vb0[:], -1.0), [], both("vb0") + ["vb0.a0", "vb0.b0"])
-            V(lambda v: v.tensor_scalar(T.vbz[:, 0:512:32], T.cw[:], 1.0, 1.0 / 512, A.add, A.mult), ["cw"], ["vbz.a0", "vbz.b0"])
-        level_scan(3)
-        limit("s2", "mkf", A.max, [0])
-        up(2)
-        level_list(3)
-        hop(4)
-        limit("s2", "mkf", A.max, [1])
-        up(3)
-        level_scan(4)
-        limit("s1", "mka", A.min, [0])
-        up(4, [0])
-        level_list(4)
-        hop(5)
-        up(4, [1])
+        for h, s, lo, hi in halves:
+            mm(h, ("qu", "su"), 0, (qx, sx), lo, 128, ["qu", "su", qx + s])
+        mm(2, ("qu", "su"), 0, (qx, sx), 0, C, ["qu", "su"] + both(qx))
+        if first:
+            o = level_scan(r, 1)
+            more_constants(0)
+            level_list(o, 1)
+            hop(r, 2)
+        for h, s, lo, hi in halves:
+            V(lambda v: v.tensor_tensor(T.wn[:, lo:hi], bank(h, 128), T.cwin[:, lo:hi], A.max), ["ps%d" % h, "cwin"], ["wn" + s])
+        o = level_scan(r, 2)
+        V(lambda v: v.tensor_tensor(T.a0[:], pick("wn", "l0"), T.idm[:], A.subtract), both("wn") + ["l0", "idm"], ["a0"])
+        level_list(o, 2)
+        window("a0", 0)
+        hop(r, 3)
+        if first:
+            more_constants(1)
+        mm(3, ("qp", "sp"), 0, (qx, sx), 0, C, ["qp", "sp"] + both(qx))
+        grow("a1", "a0", "l0")
+        if first:
+            more_constants(2)
+        window("a1", 1)
+        S(lambda q: q.activation(T.sw[:, 0:C], bank(2), F.Copy), ["ps2"], ["sw.a"])
+        o = level_scan(r, 3)
+        grow("a2", "a1", "l1")
+        level_list(o, 3)
+        window("a2", 2)
+        hop(r, 4)
+        turn(T.n3t[:], T.n3[:], ["n3"], ["n3t"])
+        grow("fw1", "a2", "l2")
+        V(lambda v: v.tensor_tensor(T.tw[:, 288:304], T.n3t[:, 0:256:16], T.cz[:, 1:17], A.subtract), ["n3t", "cz1", "cz2"], ["d8"])
+        turn(T.tw[:, 16:272], T.fw1[:, 0:C], ["fw1"], ["tw"])
+        o = level_scan(r, 4)
+        S(lambda q: q.activation(T.yy[:], pick("tw", "lc", 304), F.Copy), ["tw", "tw0", "tw1", "d8", "lc"], ["yy"])
+        level_list(o, 4)
+        S(lambda q: q.activation(T.abf[:], T.fw1[:, 0:C], F.Identity, bias=col(NOKEY)), ["fw1", "c2"], ["abf"])
+        turn(T.fw1[:, C:544], T.tw[:, 0:288], ["tw", "tw0", "tw1"], ["fw1p"])
+        hop(r, 5)
+        turn(T.b0[:], T.yy[:], ["yy"], ["b0"])
+        turn(T.ta[:, 16:272], T.abf[:], ["abf"], ["ta"])
+        window("b0", 0)
+        S(lambda q: q.activation(T.sw[:, C:2 * C], bank(3), F.Copy), ["ps3"], ["sw.b"])
+        V(lambda v: v.tensor_copy(T.ta[:, 32:273:16], T.cz[:, 1:17]), ["cz1", "cz2", "ta"], ["tac"])
+        o = level_scan(r, 5)
+        grow("b1", "b0", "l4")
+        level_list(o, 5)
+        window("b1", 1)
+        hop(r, 6)
+        turn(T.fw2[:, 0:C], T.ta[:, 17:273], ["ta", "tac"], ["fw2"])
+        grow("b2", "b1", "l5")
         for b in range(4):
-            if r == 0:
+            if first:
                 V(lambda v: v.quantize_mx(T.qe[:, 128 * b:128 * b + 128], T.se[:, 128 * b:128 * b + 128], T.et[:, 3 - b:515 - b]), ["et"], ["qe%d" % b])
             if b < 2:
-                mm(1 + b, ("qe", "se"), 128 * b, (qx, sx), 0, C, ["qe%d" % b] + both(qx))
-        limit("s1", "mka", A.min, [1])
-        up(5, [0])
-        level_scan(5)
-        up(5, [1])
-        if r == 0:
-            V(lambda v: v.memset(T.vb1[:], -1.0), [], both("vb1") + ["vb1.a0", "vb1.b0"])
-        level_list(5)
-        hop(6)
-        up(6)
-        where[0] = where[1] = "lid"
-        for i in range(9):
-            if i < 8:
-                d_pick(0, i)
-            if i == 0:
-                d_pick(1, 0)
-                unpack(0, 1, "fo", 1.0, "fo.0")
-                unpack(1, 2, "fo", 1.0, "fo.1")
-            if i > 0:
-                d_keep(1, i - 1)
-            if i < 8:
-                d_move(0, i)
-            if i > 0:
-                d_list(1, i - 1, lp, lb)
-            if i == 7:
-                send(to, T[zp][:], T[lp][:], "arp%d" % r, both(lp))
-                S(lambda q: q.activation(T.vb0[:, 0:512:32], T.fw[:], F.Copy), ["fw"], ["vb0.a0", "vb0.b0"])
-            if i == 8:
-                send(to, T[zb][:, 8:16], T[lb][:, 8:16], "arc%d" % r, [lb + ".b"])
-                break
-            d_keep(0, i)
-            if i > 0:
-                d_pick(1, i)
-            d_list(0, i, lp, lb)
-            if i == 7:
-                send(to, T[zb][:, 0:8], T[lb][:, 0:8], "arb%d" % r, [lb + ".a"])
-            d_move(1, i)
-            if i == 0:
-                for b in range(4):
-                    mm([6, 7, 3, 5][b], ("qe", "se"), 128 * b, (lq, ls), 0, C, ["qe%d" % b, lq])
-            if 2 <= i <= 5:
-                unpack(i - 2, [6, 7, 3, 5][i - 2], "fa", 0.5, "fa.%d" % (i - 2))
-            if i == 6:
-                mates_pick()
-            if r == 0 and i == 5:
-                V(lambda v: v.tensor_copy(T.mf[:], T.mti[:]), ["mti"], ["mf"])
-                V(lambda v: v.tensor_scalar(T.fw[:], T.nxi[:], 1.0, 1.0 / 512, A.add, A.mult), ["nxi"], ["fw"])
-            if r == 0 and i == 6:
-                V(lambda v: v.tensor_tensor(T.mmin[:], T.mf[:], T.cw[:], A.min), ["mf", "cw"], ["mmin"])
-                V(lambda v: v.tensor_tensor(T.mmax[:], T.mf[:], T.cw[:], A.max), ["mf", "cw"], ["mmax"])
-            if r == 0 and i == 7:
-                V(lambda v: v.tensor_copy(T.lmin[:], T.mmin[:]), ["mmin"], ["lmin"])
-                V(lambda v: v.tensor_copy(T.lmax[:], T.mmax[:]), ["mmax"], ["lmax"])
-        halves = [(0, ".a", 0, 128), (1, ".b", 128, 256)]
-        for h, s, lo, hi in halves:
-            for t in range(4):
-                S(lambda q: q.activation(T.zg[:, C * t + lo:C * t + hi], T.fa[:, C * t:C * t + C].indirect(T[zp][:, 8 * h:8 * h + 8]), F.Copy),
-                  ["fa.%d" % t, zp], ["zg.%d%s" % (t, s)])
-        for h, s, lo, hi in halves:
-            V(lambda v: v.tensor_copy(T.sb[:, lo:hi], half("sw", lb, h)), both("sw") + [lb + s], ["sb" + s])
-        for h, s, lo, hi in halves:
-            V(lambda v: v.tensor_tensor(T.xm[:, lo:hi], half("sb", "lmax", h), T.mkf[:, lo:hi], A.max), both("sb") + ["lmax", "mkf"], ["xm" + s])
-        for h, s, lo, hi in halves:
-            V(lambda v: v.tensor_tensor(T.cb0[:, 2 * lo + 1:2 * hi:2], half("sb", "lmin", h), T.xm[:, lo:hi], A.is_le), both("sb") + ["lmin", "xm" + s], ["cb0" + s])
-        for h, s, lo, hi in halves:
-            V(lambda v: v.tensor_tensor_scan(T.vb0[:, 2 * lo + 1:2 * hi:2], T.fm[:, lo:hi], T.cb0[:, 2 * lo + 1:2 * hi:2], 0.0, A.max, A.subtract), ["fm", "cb0" + s], ["vb0" + s])
-        for h, s, lo, hi in halves:
-            d_keep(h, 6)
-        for h, s, lo, hi in halves:
-            V(lambda v: v.tensor_scalar(T.l0[:, 8 * h:8 * h + 8], T.rb0[:, 2 * lo + 31:2 * hi:32], 512.0, -1.0, A.mult, A.add), ["rb0" + s], ["l0" + s])
-        if r < 2:
-            S(lambda q: q.activation(T.n0[:], pick("idn", "l0"), F.Copy), ["idn"] + both("l0"), ["n0"])
-            hop(1)
-            S(lambda q: q.activation(T.fw[:], T.rb0[:, 31:512:32], F.Copy), both("rb0"), ["fw"])
+                mm(b, ("qe", "se"), 128 * b, (qx, sx), 0, C, ["qe%d" % b] + both(qx))
+        for b in range(4):
+            mm(4 + b, ("qe", "se"), 128 * b, (lq, ls), 0, C, ["qe%d" % b, lq])
+        o = level_scan(r, 6)
+        window("b2", 2)
+        level_list(o, 6)
+        S(lambda q: q.activation(T.s1[:], T.sw[:, 0:C], F.Identity, scale=score, bias=col(KEYS)), ["sw.a", "e5", "c1"], ["s1"])
+        if first:
+            more_constants(3)
+        grow("b3", "b2", "l6")
+        turn(T.fw2[:, C:544], T.ta[:, 1:289], ["ta", "ta0", "tac"], ["fw2p"])
+        hop(r, 7)
+        V(lambda v: v.tensor_tensor(T.od[:], pick("b3", "l3"), T.s1[:], A.subtract), ["b3", "l3", "s1"], ["od"])
+        S(lambda q: q.activation(T.s2[:], pick("sw", "l2s", 512), F.Identity, scale=score, bias=col(EDGE)), both("sw") + ["l2s0", "l2s1", "e5", "c3"], ["s2"])
+        V(lambda v: v.tensor_tensor(T.ev[:], T.b3[:], T.s1[:], A.subtract), ["b3", "s1"], ["ev"])
+        turn(T.xt[:, 0:512:2], T.od[:], ["od"], ["xt0"])
+        S(lambda q: q.activation(T.xt[:, 0:513:32], T.cz[:, 0:17], F.Copy), ["cz0", "cz1", "cz2"], ["xt0"])
+        turn(T.xt[:, 1:512:2], T.ev[:], ["ev"], ["xt1"])
+        o = level_scan(r, 7)
+        unpack(0, 4, "fa", 0.5, "fa.0")
+        unpack(1, 5, "fa", 0.5, "fa.1")
+        V(lambda v: v.tensor_scalar(T.nf2[:, 0:496], T.xt[:, 0:496], 0.0, None, A.is_le), ["xt0", "xt1"], ["nf2"])
+        V(lambda v: v.tensor_scalar(T.sm[:, 8:9], col(INV), -UNIT, None, A.mult), ["c4"], ["sm8"]) if first else None
+        V(lambda v: v.tensor_tensor_scan(T.rc[:, 0:496], T.nf2[:, 0:496], T.xt[:, 17:513], 0.0, A.mult, A.add), ["nf2", "xt0", "xt1"], ["rc"])
+        V(lambda v: v.tensor_scalar(T.dm[:], T[o][:, 15:256:16], T.sm[:, 8:9], None, A.mult), [o, "sm8"], ["dm"])
+        for e in range(2):
+            V(lambda v: v.tensor_scalar(T.lq2[:, e:16:2], T.rc[:, 15 + 32 * e:496:64], 1.0 / UNIT, col(OFF0 + e), A.mult, A.add), ["rc", "c5", "c6"], ["lq2%d" % e])
+        V(lambda v: v.tensor_tensor(T.df[:], T.dm[:], T.ch[:, 0:16], A.add), ["dm", "ch"], ["df"])
+        S(lambda q: q.activation(T.xr[:], pick("fw2", "lq2", 544), F.Copy), ["fw2", "fw2p", "lq20", "lq21"], ["xr"])
+        V(lambda v: v.tensor_tensor(T.fl[:], pick("fw1", "lq2", 544), T.s2[:], A.is_le), ["fw1", "fw1p", "lq20", "lq21", "s2"], ["fl"])
+        turn(T.rt[:], T.xr[:], ["xr"], ["rt"])
+        S(lambda q: q.activation(T.rt[:, 6:256:16], T.df[:], F.Copy), ["df"], ["rt"])
+        turn(T.zt[:, 16:272], T.fl[:], ["fl"], ["zt"])
+        V(lambda v: v.tensor_tensor_scan(T.rb[:, 0:250], T.zt[:, 15:265], T.rt[:, 6:256], 0.0, A.mult, A.add), ["zt", "zt0", "rt"], ["rb"])
+        S(lambda q: q.activation(T.rt[:, 7:256:16], T.df[:], F.Copy, scale=0.0), ["df"], ["rt"])
+        V(lambda v: v.tensor_scalar(L(lb), T.rb[:, 9:250:16], 1.0 / UNIT, -1.0, A.mult, A.add), ["rb"], [lb])
+        send(to, T[zb][:], L(lb), "arb%d" % r, [lb])
+        V(lambda v: v.tensor_tensor_scan(T.rp[:, 0:249], T.zt[:, 15:264], T.rt[:, 7:256], 0.0, A.mult, A.add), ["zt", "zt0", "rt"], ["rp"])
+        unpack(2, 6, "fa", 0.5, "fa.2")
+        unpack(3, 7, "fa", 0.5, "fa.3")
+        if first:
+            V(lambda v: v.tensor_copy(T.tj[:], T.ii[:]), ["ii", "dl"], ["tj", "tj2"])
+        V(lambda v: v.tensor_scalar(L(lp), T.rp[:, 8:249:16], 1.0 / UNIT, -1.0, A.mult, A.add), ["rp"], [lp])
+        send(to, T[zp][:], L(lp), "arp%d" % r, [lp])
         for t in (2, 3):
             mm(4 + t, ("qe", "se"), 128 * t, (qx, sx), 0, C, ["qe%d" % t] + both(qx))
+        if first:
+            more_constants(4)
+            more_constants(5)
+        V(lambda v: v.tensor_tensor(T.yn[:], pick("sw", lb), T.sg[:], A.mult), ["sw.a", lb, "sg"], ["yn"])
+        S(lambda q: q.activation(T.yp[:], T.yn[:], F.Copy, scale=-1.0), ["yn"], ["yp"])
+        unpack(0, 0, "fo", 1.0, "fo.0")
+        unpack(1, 1, "fo", 1.0, "fo.1")
+        V(lambda v: v.tensor_tensor(T.xf[:], pick("yn", "lm"), T.yp[:], A.is_gt), ["yn", "yp", "lm"], ["xf"])
+        V(lambda v: v.tensor_tensor_scan(T.xs[:], T.dl[:], T.xf[:], 0.0, A.mult, A.add), ["dl", "xf"], ["xs"])
+        V(lambda v: v.tensor_scalar(T.ex[:, 1:32:2], T.xs[:, 15:256:16], T.thr[:, 0:1], None, A.is_ge), ["xs", "thr"], ["ex1"])
+        V(lambda v: v.tensor_tensor_scan(T.exo[:], T.ex[:], T.exd[:], 0.0, A.mult, A.add), ["ex0", "ex1", "exd0", "exd1"], ["exo"])
+        V(lambda v: v.tensor_copy(T.lsg[:], T.exo[:, 1:32:2]), ["exo"], ["lsg"])
+        def first_terms(h, s, lo, hi):
+            for t in range(4):
+                S(lambda q: q.activation(T.zg[:, C * t + lo:C * t + hi], T.fa[:, C * t:C * t + C].indirect(T[zb][:, 8 * h:8 * h + 8]), F.Copy),
+                  ["fa.%d" % t, zb], ["zg.%d%s" % (t, s)])
+        first_terms(*halves[0])
+        first_terms(*halves[1])
+        old, new = n_name(r, 0), n_name(r + 1, 0)
+        if r < 2:
+            S(lambda q: q.activation(T[new][:], pick(old, "lsg"), F.Copy), [old, "lsg"], [new])
         def z_ready(h, s, lo, hi):
             quant("qz", "sz", "z", "qz" + s, ["z.%d%s" % (t, s) for t in range(4)], lo)
             for k in range(4):
@@ -415,14 +399,14 @@ def rank_program(g, core, T, topo):
 
         for h, s, lo, hi in halves:
             for t in range(4):
-                V(lambda v: v.tensor_tensor(T.z[:, 4 * lo + t:4 * hi:4], T.fa[:, C * t:C * t + C].indirect(T[zb][:, 8 * h:8 * h + 8]), T.zg[:, C * t + lo:C * t + hi], A.add),
-                  ["fa.%d" % t, zb + s, "zg.%d%s" % (t, s)], ["z.%d%s" % (t, s)])
+                V(lambda v: v.tensor_tensor(T.z[:, 4 * lo + t:4 * hi:4], T.fa[:, C * t:C * t + C].indirect(T[zp][:, 8 * h:8 * h + 8]), T.zg[:, C * t + lo:C * t + hi], A.add),
+                  ["fa.%d" % t, zp, "zg.%d%s" % (t, s)], ["z.%d%s" % (t, s)])
                 if h == 1 and t == 0:
                     z_ready(*halves[0])
         z_ready(*halves[1])
         if r < 2:
-            level_scan(1)
-            level_list(1)
+            o = level_scan(r + 1, 0)
+            level_list(o, 0)
         else:
             quant("qv", "sv", "vt", "qv", ["vt"])
         xn = "x%d" % (r + 1)
@@ -431,14 +415,14 @@ def rank_program(g, core, T, topo):
 
         for h, s, lo, hi in halves:
             for t in (2, 3):
-                S(lambda q: q.activation(T.zg[:, C * t + lo:C * t + hi], T.hh[:, C * t:C * t + C].indirect(T[lb][:, 8 * h:8 * h + 8]), F.Copy),
-                  both("hh.%d" % t) + [lb + s], ["zg.%d%s" % (t, s)])
+                S(lambda q: q.activation(T.zg[:, C * t + lo:C * t + hi], T.hh[:, C * t:C * t + C].indirect(L(lb, 8 * h, 8 * h + 8)), F.Copy),
+                  both("hh.%d" % t) + [lb], ["zg.%d%s" % (t, s)])
         if r < 2:
-            hop(2)
+            hop(r + 1, 1)
         for h, s, lo, hi in halves:
             for t in (0, 1):
-                V(lambda v: v.tensor_tensor(T[xn][:, 4 * lo + t:4 * hi:4], T.hh[:, C * t:C * t + C].indirect(T[lb][:, 8 * h:8 * h + 8]), T.fo[:, C * t + lo:C * t + hi], A.add),
-                  both("hh.%d" % t) + ["fo.%d" % t, lb + s], ["%s.%d%s" % (xn, t, s)])
+                V(lambda v: v.tensor_tensor(T[xn][:, 4 * lo + t:4 * hi:4], T.hh[:, C * t:C * t + C].indirect(L(lb, 8 * h, 8 * h + 8)), T.fo[:, C * t + lo:C * t + hi], A.add),
+                  both("hh.%d" % t) + ["fo.%d" % t, lb], ["%s.%d%s" % (xn, t, s)])
         for h, s, lo, hi in halves:
             for t in (2, 3):
                 V(lambda v: v.tensor_tensor(T[xn][:, 4 * lo + t:4 * hi:4], T.zg[:, C * t + lo:C * t + hi], T.ps[:, 512 * (4 + t) + lo:512 * (4 + t) + hi], A.add),
@@ -446,9 +430,13 @@ def rank_program(g, core, T, topo):
                 if h == 1 and t == 2:
                     x_ready(*halves[0])
         x_ready(*halves[1])
-        if r == 2:
-            S(lambda q: q.activation(T.nff[:], pick("idn", "l0"), F.Identity, bias=-1.0, scale=512.0), ["idn"] + both("l0"), ["nff"])
-    op("y", lambda q: q.dma_start(T.nf[:], T.nff[0:128:16, :]), ["nff"], [], "dnf", 16)
+        if r < 2:
+            o = level_scan(r + 1, 1)
+            level_list(o, 1)
+            hop(r + 1, 2)
+        else:
+            S(lambda q: q.activation(T.a0[:], pick(old, "lsg"), F.Identity, bias=-1.0, scale=1.0 / UNIT), [old, "lsg"], ["a0"])
+    op("y", lambda q: q.dma_start(T.nf[:], T.a0[0:128:16, :]), ["a0"], [], "dnf", 16)
     op("y", lambda q: q.dma_start(T.oc[:], T.qx3[:, 0:C].bitcast(U8)), both("qx3"), [], "doc", 16)
     for h in range(2):
         mm(6 + h, ("qv", "sv"), 0, ("qx3", "sx3"), 128 * h, 128, ["qv", "qx3" + [".a", ".b"][h]])

@@ -4,24 +4,25 @@ STEP = [1, 2, 4]
 C = 256
 R3 = 3
 CODE = "float8_e4m3fn_x4"
-UNIT = 2.0 ** 71
+UNIT = 2.0 ** 80
 BIG = 1.0e29
-KEY = 1024.0 * UNIT
-LISTS = "l0 l1 l2 l3 l4 l5 l6 lp0 lp1 lp2 lb0 lb1 lb2".split()
-SCRATCH = {"ps": ("psum", [128, 4096], "float32")}
+KEY = 1024.0
+CUT = 192
+LISTS = "l0 l1 l2 l3 l4 l5 l6 lp0 lp1 lp2 lb0 lb1 lb2 lmin lmax lc l2s lq2 lsg ld".split()
+SCRATCH = {"ps": ("psum", [128, 4096], "float32"), "xt": ("sbuf", [128, 16, 40], "bfloat16")}
 for _names, _cols, _type in [
-        ("ut vt", 512, "bfloat16"), ("qu0 qu qp qv", 128, CODE), ("su0 su sp sv", 128, "uint8"), ("wq qe", 512, CODE), ("wp se", 512, "uint8"),
-        ("ones et", 520, "bfloat16"), ("nxi mti pi ti", 16, "int32"), ("e5 col bias kk cw dm df thr sm", 16, "float32"), ("ex exd exo", 32, "float32"),
-        ("tj ii d1 idm cwin wn wa a0 a1 a2 b0 b1 b2 b3 yy s1 s2 yn yp sg yt", 256, "float32"), ("sw", 512, "float32"), ("tw", 304, "float32"), ("fw1", 544, "float32"),
-        ("idn dl nsa nsb n3t abf od ev fl xr rt rb rp xf xs", 256, "bfloat16"), ("ta", 304, "bfloat16"), ("fw2 xt", 544, "bfloat16"), ("nf2 rc", 512, "bfloat16"), ("zt", 272, "bfloat16"),
-        ("cz ch", 32, "bfloat16"), ("lu lv lm lc l2s lq2 lsg", 16, "uint16"), ("ll", 16 * len(LISTS), "uint16"),
+        ("ut vt", 512, "bfloat16"), ("qu0 qu qv", 128, CODE), ("su0 su sv", 128, "uint8"), ("wq qe", 512, CODE), ("wp se", 512, "uint8"),
+        ("ones et", 520, "bfloat16"), ("nxi mti pi ti", 16, "int32"), ("e5 bias cw dm df t16 d16 e16 g16 mlo mhi", 16, "float32"), ("col ex exd exo", 32, "float32"),
+        ("ii idm cwin wn wa a0 a1 a2 b0 b1 b2 b3 b4 yy s1 s2 sb slo yt", 256, "float32"), ("sw fw1", 768, "float32"), ("tw", 288, "float32"),
+        ("idn dl nsa nsb n3t abf od ev fl xr rt rb rp xf xs nf2 dd rc", 256, "bfloat16"), ("fw2", 768, "bfloat16"), ("zt", 272, "bfloat16"),
+        ("cz ch h16", 16, "bfloat16"), ("lu", 16, "uint16"), ("ll", 16 * len(LISTS), "uint16"),
         ("fa fo zg z hh x0 x1 x2 x3", 1024, "bfloat16"), ("qz qx0 qx1 qx2 qx3 lq0 lq1 lq2c", 256, CODE), ("sz sx0 sx1 sx2 sx3 ls0 ls1 ls2", 256, "uint8"),
         ("zp0 zp1 zp2 zb0 zb1 zb2", 16, "uint16"),
         ("f0 f1 n1 n2 n3 n4 n5 n6 n7", 256, "bfloat16")]:
     for _n in _names.split():
         SCRATCH[_n] = ("sbuf", [128, _cols], _type)
-DMAS = ["dx", "dnx", "dmt", "du", "dwc", "dws", "dv", "doc", "dos0", "dos1", "dos2", "dos3", "dy0", "dy1", "dnf"]
-SEMAPHORES = ["cv", "cs", "ct", "cg", "sent"] + DMAS + ["%s%d" % (n, i) for n in ("arq", "arp", "arb") for i in range(3)]
+DMAS = ["dx", "dnx", "dmt", "du", "dwc", "dws", "dv", "doc", "dos0", "dos1", "dos2", "dos3", "dy0", "dy1", "dnf", "dsw", "dfw1", "dfw2", "dabf"]
+SEMAPHORES = ["cv", "cs", "ct", "cg", "sent"] + DMAS + ["%s%d" % (n, i) for n in ("arq", "zp", "zb") for i in range(3)]
 
 
 def make_issue(g, T):
@@ -60,11 +61,12 @@ def make_issue(g, T):
             evs += [ev for ev, o in readers.get(k, [])]
         need(e, evs)
 
-    def op(e, call, reads=(), writes=(), sem=None, inc=1):
+    def op(e, calls, reads=(), writes=(), sem=None, inc=1):
         wait_for(e, reads, writes)
         sem = sem or "c" + e
-        call(queue[e]).then_inc(T.sem[sem], inc)
-        count[sem] = count.get(sem, 0) + inc
+        for call in calls if isinstance(calls, list) else [calls]:
+            call(queue[e]).then_inc(T.sem[sem], inc)
+            count[sem] = count.get(sem, 0) + inc
         ev = (sem, count[sem])
         clock[ev] = dict(known[e])
         for k in reads:
@@ -109,6 +111,9 @@ def rank_program(g, core, T, topo):
     def G(call, reads, writes):
         op("g", call, reads, writes)
 
+    def copies(pairs, reads, writes, sem):
+        op("y", [(lambda q, o=o, i=i: q.dma_start(o, i)) for o, i in pairs], reads, writes, sem, 16)
+
     def both(name):
         return [name + ".a", name + ".b"]
 
@@ -123,106 +128,121 @@ def rank_program(g, core, T, topo):
     def quant(q, s, tile, key, reads, lo=0, n=128):
         V(lambda v: v.quantize_mx(T[q][:, lo:lo + n], T[s][:, lo:lo + n], T[tile][:, 4 * lo:4 * lo + 4 * n]), reads, [key])
 
-    def L(lst, a=0, b=16):
+    def L(lst, a=0, b=16, step=1):
         if lst in LISTS:
-            return T.ll[:, 16 * LISTS.index(lst) + a:16 * LISTS.index(lst) + b]
+            return T.ll[:, 16 * LISTS.index(lst) + a:16 * LISTS.index(lst) + b:step]
         return T[lst][:, a:b]
 
     def pick(win, lst, n=C):
         return T[win][:, 0:n].indirect(L(lst))
 
-    def col(k):
-        return T.col[:, k:k + 1]
-    STEPS, KEYS, NOKEY, EDGE, INV, OFF0, OFF1, LOW, LANE, SLOT = range(10)
+    names = []
+
+    def col(name):
+        if name not in names:
+            names.append(name)
+        return T.col[:, names.index(name):names.index(name) + 1]
+
+    def line(name, src, keys, a, b):
+        S(lambda s: s.activation(col(name), src, F.Identity, scale=a, bias=b), keys, [name])
+
+    def whole(out, pattern, base, key):
+        G(lambda q: q.iota(out, pattern, base, 0, allow_small_or_imprecise_dtypes=True), [], [key])
+
+    def tiles(which):
+        for b in which:
+            V(lambda v: v.quantize_mx(T.qe[:, 128 * b:128 * b + 128], T.se[:, 128 * b:128 * b + 128], T.et[:, 3 - b:515 - b]), ["et"], ["qe%d" % b])
 
     op("y", lambda q: q.dma_start(T.nxi[:], T.nx[:]), [], ["nxi"], "dnx", 16)
     op("s", lambda q: q.dma_start(T.x0[:], T.x[:]), [], ["x0"], "dx", 16)
     op("y", lambda q: q.dma_start(T.ut[:], T.u[:]), [], ["ut"], "du", 16)
     op("y", lambda q: q.dma_start(T.mti[:], T.mt[:]), [], ["mti"], "dmt", 16)
+
+    G(lambda q: q.iota(T.pi[:, 0:1], [[0, 1]], 0, 1), [], ["pi"])
+    whole(T.cw[:], [[16, 16]], 0, "k16")
+    whole(T.ii[:], [[1, 256]], 1, "ii")
+    whole(T.t16[:], [[1, 16]], 0, "t16")
+    V(lambda v: v.memset(T.ones[:], 1.0), [], ["ones"])
+    G(lambda q: q.affine_select(T.et[:], T.ones[:], [[-1, 520]], A.is_equal, 0.0, 3, 4), ["ones"], ["et"])
+    for view, n, key in [(T.tw[:, 8:16], 8, "tw0"), (T.tw[:, 280:288], 8, "tw1"), (T.zt[:, 0:16], 16, "zt0"), (T.ex[:, 0:32:2], 16, "ex0")]:
+        whole(view, [[0, n]], 0, key)
+    for k, m in enumerate((1, 2, 4, 8, 16, 15, 31)):
+        V(lambda v: v.tensor_scalar(T.ti[:, k:k + 1], T.pi[:, 0:1], m, None, A.bitwise_and), ["pi"], ["ti%d" % k])
+    ti = ["ti%d" % k for k in range(7)]
+    V(lambda v: v.tensor_scalar(T.e5[:, 0:5], T.ti[:, 0:5], 0.0, None, A.is_equal), ti, ["e5"])
+    V(lambda v: v.tensor_copy(T.e5[:, 5:7], T.ti[:, 5:7]), ti, ["e8"])
+    score, even, lane = T.e5[:, 3:4], T.e5[:, 4:5], T.e5[:, 5:6]
+    S(lambda s: s.activation(T.idn[:], T.ii[:], F.Copy, scale=UNIT), ["ii"], ["idn"])
+    line("steps", score, ["e5"], -UNIT, UNIT)
+    line("low", score, ["e5"], -BIG, 0.0)
+    line("key", score, ["e5"], -KEY * UNIT, KEY * UNIT)
+    line("i1", T.e5[:, 6:7], ["e8"], UNIT, UNIT)
+    S(lambda s: s.activation(T.bias[:, 0:3], T.e5[:, 0:3], F.Identity, scale=BIG, bias=-BIG), ["e5"], ["bias0"])
+    line("lc0", score, ["e5"], 15.0 / 16, 1.0 / 16)
+    line("lc1", score, ["e5"], 16.0, 0.0)
+    line("lc2", score, ["e5"], -248.0, 120.0)
+    S(lambda s: s.activation(T.bias[:, 4:7], T.bias[:, 0:3], F.Identity, bias=col("key")), ["bias0", "key"], ["bias"])
+    S(lambda s: s.activation(T.bias[:, 8:11], T.e5[:, 0:3], F.Identity, scale=col("key"), accum_out=col("keys0")), ["e5", "key"], ["keys0"])
+    V(lambda v: v.tensor_scalar(col("last"), lane, 15.0, None, A.is_equal), ["e8"], ["last"])
+    V(lambda v: v.tensor_scalar(T.d16[:], T.t16[:], lane, None, A.subtract), ["t16", "e8"], ["d16"])
+    V(lambda v: v.tensor_scalar(L("ld"), T.t16[:], 0.0, lane, A.mult, A.add), ["t16", "e8"], ["ld"])
+    V(lambda v: v.tensor_scalar(T.e16[:], T.d16[:], 1.0, 1023.0, A.is_equal, A.mult), ["d16"], ["e16"])
+    V(lambda v: v.tensor_scalar(T.g16[:], T.d16[:], 0.0, None, A.not_equal), ["d16"], ["g16"])
+    V(lambda v: v.tensor_scalar(T.lu[:, 0:8], T.cw[:, 0:8], 0.0, None, A.add), ["k16"], ["lu"])
+    V(lambda v: v.tensor_tensor(T.h16[:], T.e16[:], T.g16[:], A.add), ["e16", "g16"], ["h16"])
+    V(lambda v: v.tensor_scalar(T.exd[:, 1:32:2], T.cw[:], lane, None, A.add), ["k16", "e8"], ["exd1"])
+    V(lambda v: v.tensor_scalar(col("lane0"), lane, 0.0, -BIG, A.is_equal, A.mult), ["e8"], ["lane0"])
+    V(lambda v: v.tensor_copy(L("l0"), T.nxi[:]), ["nxi"], ["l0"])
+    V(lambda v: v.tensor_copy(T.dl[:], pick("h16", "ld", 16)), ["h16", "ld"], ["dl"])
+    line("inv", col("last"), ["last"], 1023.0 / 1024 / UNIT, 1.0 / 1024 / UNIT)
+    line("nokey", col("keys0"), ["keys0"], -1.0, 0.0)
+    S(lambda s: s.activation(T.f0[:], pick("idn", "l0"), F.Copy), ["idn", "l0"], ["f0"])
+    S(lambda s: s.activation(T.cwin[:], T.ii[:], F.Identity, scale=col("steps"), bias=col("low")), ["ii", "steps", "low"], ["cwin"])
+    copies([(T.fw2[:, C * k:C * k + C], T.idn[:]) for k in range(3)], ["idn"], ["fw2"], "dfw2")
+    copies([(T.fw1[:, C * k:C * k + C], T.ii[:]) for k in (1, 2)], ["ii"], ["fw1p"], "dfw1")
+    copies([(T.sw[:, C * k:C * k + C], T.ii[:]) for k in (1, 2)], ["ii"], ["swp"], "dsw")
     op("y", lambda q: q.dma_start(T.wq[:, 0:512].bitcast(U8), T.wc[:]), [], ["wq"], "dwc", 16)
     op("y", lambda q: q.dma_start(T.wp[:, 0:512], T.ws[:]), [], ["wp"], "dws", 16)
     op("y", lambda q: q.dma_start(T.vt[:], T.v[:]), [], ["vt"], "dv", 16)
-
-    G(lambda q: q.iota(T.pi[:, 0:1], [[0, 1]], 0, 1), [], ["pi"])
-    G(lambda q: q.iota(T.ii[:], [[1, 256]], 1, 0, allow_small_or_imprecise_dtypes=True), [], ["ii"])
-    G(lambda q: q.iota(T.cw[:], [[16, 16]], 0, 0, allow_small_or_imprecise_dtypes=True), [], ["k16"])
-    G(lambda q: q.iota(T.tj[:], [[0, 16], [1, 16]], 0, 0, allow_small_or_imprecise_dtypes=True), [], ["tj"])
-    V(lambda v: v.memset(T.ones[:], 1.0), [], ["ones"])
-    G(lambda q: q.affine_select(T.et[:], T.ones[:], [[-1, 520]], A.is_equal, 0.0, 3, 4), ["ones"], ["et"])
-    for k, m in enumerate((1, 2, 4, 8, 16, 15, 7, 31)):
-        V(lambda v: v.tensor_scalar(T.ti[:, k:k + 1], T.pi[:, 0:1], m, None, A.bitwise_and), ["pi"], ["ti%d" % k])
-    for k in range(3):
-        V(lambda v: v.memset(T.kk[:, k:k + 1], KEY * 2 ** k), [], ["kk%d" % k])
-    ti = ["ti%d" % k for k in range(8)]
-    V(lambda v: v.tensor_scalar(T.e5[:, 0:5], T.ti[:, 0:5], 0.0, None, A.is_equal), ti, ["e5"])
-    V(lambda v: v.tensor_copy(T.e5[:, 5:8], T.ti[:, 5:8]), ti, ["e8"])
-    score, even, lane = T.e5[:, 3:4], T.e5[:, 4:5], T.e5[:, 5:6]
-    V(lambda v: v.tensor_scalar(T.lu[:, 0:8], T.cw[:, 0:8], 0.0, None, A.add), ["k16"], ["lu"])
-    V(lambda v: v.tensor_scalar(T.idn[:], T.ii[:], UNIT, None, A.mult), ["ii"], ["idn"])
-    V(lambda v: v.tensor_scalar(col(STEPS), score, -UNIT, UNIT, A.mult, A.add), ["e5"], ["c0"])
-    V(lambda v: v.tensor_scalar(col(LOW), score, -BIG, None, A.mult), ["e5"], ["c7"])
-    V(lambda v: v.tensor_scalar(T.sm[:, 0:1], lane, 15.0, None, A.is_equal), ["e8"], ["sm0"])
-    V(lambda v: v.tensor_scalar(T.d1[:], T.tj[:], lane, None, A.subtract), ["tj", "e8"], ["d1"])
-    V(lambda v: v.tensor_copy(L("l0"), T.nxi[:]), ["nxi"], ["l0"])
-    S(lambda s: s.activation(T.f0[:], pick("idn", "l0"), F.Copy), ["idn", "l0"], ["f0"])
-    V(lambda v: v.tensor_scalar(T.tj[:], T.d1[:], 1.0, 1023.0, A.is_equal, A.mult), ["d1"], ["tj"])
-    V(lambda v: v.tensor_scalar(col(INV), T.sm[:, 0:1], 1023.0 / 1024 / UNIT, 1.0 / 1024 / UNIT, A.mult, A.add), ["sm0"], ["c4"])
-    V(lambda v: v.tensor_scalar(T.d1[:], T.d1[:], 0.0, None, A.not_equal), ["d1"], ["d1"])
+    tiles([0])
     quant("qu0", "su0", "ut", "qu0", ["ut"])
-    V(lambda v: v.tensor_tensor(T.dl[:], T.tj[:], T.d1[:], A.add), ["tj", "d1"], ["dl"])
     S(lambda s: s.activation(T.n1[:], pick("f0", "l0"), F.Copy), ["f0", "l0"], ["n1"])
+    tiles([1])
     V(lambda v: v.tensor_copy(T.qu[:, 0:128].bitcast(U32), T.qu0[:, 0:128].bitcast(U32).indirect(T.lu[:, 0:8])), ["qu0", "lu"], ["qu"])
     S(lambda s: s.activation(T.su[:, 0:128], T.su0[:, 0:128].indirect(T.lu[:, 0:8]), F.Copy), ["qu0", "lu"], ["su"])
     quant("qx0", "sx0", "x0", "qx0.a", ["x0"])
     quant("qx0", "sx0", "x0", "qx0.b", ["x0"], 128)
-    S(lambda s: s.activation(T.idm[:], T.ii[:], F.Identity, scale=col(STEPS)), ["ii", "c0"], ["idm"])
-    S(lambda s: s.activation(T.cwin[:], T.ii[:], F.Identity, scale=col(STEPS), bias=col(LOW)), ["ii", "c0", "c7"], ["cwin"])
+    S(lambda s: s.activation(T.idm[:], T.ii[:], F.Identity, scale=col("steps")), ["ii", "steps"], ["idm"])
 
     def more_constants(part):
         if part == 0:
-            V(lambda v: v.tensor_scalar(T.bias[:, 0:3], T.e5[:, 0:3], BIG, -BIG, A.mult, A.add), ["e5"], ["bias0"])
-            V(lambda v: v.tensor_scalar(T.kk[:, 4:7], T.kk[:, 0:3], 1.0 / UNIT, col(STEPS), A.mult, A.mult), ["kk0", "kk1", "kk2", "c0"], ["kk"])
-            V(lambda v: v.tensor_scalar(T.sm[:, 1:2], T.e5[:, 6:7], -1024.0, 7168.0, A.mult, A.add), ["e8"], ["sm1"])
-            V(lambda v: v.tensor_tensor(T.bias[:, 4:7], T.bias[:, 0:3], T.kk[:, 4:7], A.add), ["bias0", "kk"], ["bias"])
-            V(lambda v: v.tensor_tensor(col(KEYS), T.sm[:, 1:2], col(STEPS), A.mult), ["sm1", "c0"], ["c1"])
+            for e in range(2):
+                S(lambda s: s.activation(T.cz[:, e:16:2], T.cw[:, 0:16:2], F.Identity, scale=UNIT, bias=col("i1")), ["k16", "i1"], ["cz%d" % e])
+            for h, s, lo, hi in halves:
+                V(lambda v: v.tensor_scalar(L("lc", 8 * h, 8 * h + 8), T.cw[:, 8 * h:8 * h + 8], col("lc0"), col("lc%d" % (1 + h)), A.mult, A.add), ["k16", "lc0", "lc1", "lc2"], ["lc" + s])
         if part == 1:
-            V(lambda v: v.tensor_scalar(T.lv[:, 0:8:2], T.cw[:, 0:8:2], 16.0, None, A.add), ["k16"], ["lv0"])
-            V(lambda v: v.tensor_scalar(T.lv[:, 1:8:2], T.cw[:, 1:8:2], -16.0, None, A.add), ["k16"], ["lv1"])
-            V(lambda v: v.tensor_scalar(col(NOKEY), col(KEYS), -1.0, None, A.mult), ["c1"], ["c2"])
-            V(lambda v: v.tensor_scalar(T.sm[:, 2:3], T.e5[:, 7:8], 1.0, None, A.add), ["e8"], ["sm2"])
-            V(lambda v: v.memset(T.cz[:, 0:1], UNIT), [], ["cz0"])
-            V(lambda v: v.tensor_copy(T.qp[:, 0:128].bitcast(U32), T.qu0[:, 0:128].bitcast(U32).indirect(T.lv[:, 0:8])), ["qu0", "lv0", "lv1"], ["qp"])
-            S(lambda s: s.activation(T.sp[:, 0:128], T.su0[:, 0:128].indirect(T.lv[:, 0:8]), F.Copy), ["qu0", "lv0", "lv1"], ["sp"])
-            for e in range(2):
-                V(lambda v: v.tensor_scalar(T.cz[:, 1 + e:17:2], T.cw[:, 0:16:2], T.sm[:, 2:3], UNIT, A.add, A.mult), ["k16", "sm2"], ["cz%d" % (1 + e)])
+            line("keys", col("keys0"), ["keys0", "lane0"], 1.0, col("lane0"))
+            line("edge0", col("last"), ["last"], -2.0 * BIG / UNIT, BIG / UNIT)
+            line("w0", even, ["e5"], -272.0, 272.0)
+            line("w1", even, ["e5"], 496.0, 0.0)
         if part == 2:
-            V(lambda v: v.tensor_scalar(T.sm[:, 3:4], score, 15.0 / 16, 1.0 / 16, A.mult, A.add), ["e5"], ["sm3"])
-            V(lambda v: v.tensor_scalar(T.sm[:, 4:5], score, -272.0, 288.0, A.mult, A.add), ["e5"], ["sm4"])
-            V(lambda v: v.memset(T.tw[:, 0:16], 0.0), [], ["tw0"])
-            V(lambda v: v.memset(T.tw[:, 272:288], 0.0), [], ["tw1"])
-            V(lambda v: v.tensor_scalar(T.lc[:], T.cw[:], T.sm[:, 3:4], T.sm[:, 4:5], A.mult, A.add), ["k16", "sm3", "sm4"], ["lc"])
-            V(lambda v: v.memset(T.ta[:, 0:16], 0.0), [], ["ta0"])
-            V(lambda v: v.memset(T.ta[:, 272:304], 0.0), [], ["tac"])
-            V(lambda v: v.memset(T.zt[:, 0:16], 0.0), [], ["zt0"])
-        if part == 3:
-            V(lambda v: v.tensor_scalar(col(OFF0), even, -256.0, 255.0, A.mult, A.add), ["e5"], ["c5"])
-            V(lambda v: v.tensor_scalar(col(OFF1), even, 288.0, -1.0, A.mult, A.add), ["e5"], ["c6"])
-            V(lambda v: v.tensor_scalar(T.sm[:, 5:6], even, -272.0, 272.0, A.mult, A.add), ["e5"], ["sm5"])
-            V(lambda v: v.tensor_scalar(T.sm[:, 6:7], even, 240.0, None, A.mult), ["e5"], ["sm6"])
-            V(lambda v: v.tensor_scalar(T.sm[:, 7:8], T.sm[:, 0:1], -2.0 * BIG, BIG, A.mult, A.add), ["sm0"], ["sm7"])
+            line("edge", col("edge0"), ["edge0", "steps"], col("steps"), 0.0)
+            line("off0", even, ["e5"], -256.0, 255.0)
+            line("off1", even, ["e5"], 512.0, -1.0)
+            line("ninv", col("inv"), ["inv"], -UNIT, 0.0)
             for e in range(2):
-                V(lambda v: v.tensor_scalar(T.l2s[:, e:16:2], T.cw[:, e:16:2], T.sm[:, 5 + e:6 + e], lane, A.add, A.add), ["k16", "sm5", "sm6", "e8"], ["l2s%d" % e])
-            V(lambda v: v.tensor_scalar(col(EDGE), T.sm[:, 7:8], 1.0 / UNIT, col(STEPS), A.mult, A.mult), ["sm7", "c0"], ["c3"])
-            V(lambda v: v.tensor_scalar(T.exd[:, 1:32:2], T.cw[:], lane, None, A.add), ["k16", "e8"], ["exd1"])
-            V(lambda v: v.tensor_scalar(T.ch[:, 0:16], T.exd[:, 1:32:2], 1.0, UNIT, A.add, A.mult), ["exd1"], ["ch"])
+                V(lambda v: v.tensor_scalar(L("l2s", e, 16, 2), T.cw[:, e:16:2], col("w%d" % e), lane, A.add, A.add), ["k16", "w%d" % e, "e8"], ["l2s%d" % e])
+        if part == 3:
+            S(lambda s: s.activation(T.xt[:, :, 32], T.cz[:], F.Copy), ["cz0", "cz1"], ["xtc"])
+            S(lambda s: s.activation(T.ch[:], T.exd[:, 1:32:2], F.Identity, scale=UNIT, bias=UNIT), ["exd1"], ["ch"])
+            line("thr", col("last"), ["last"], -511.5, 512.0)
         if part == 4:
-            V(lambda v: v.tensor_copy(T.lm[:], T.mti[:]), ["mti"], ["lm"])
-            V(lambda v: v.tensor_tensor(T.exd[:, 0:32:2], T.mti[:], T.exd[:, 1:32:2], A.subtract), ["mti", "exd1"], ["exd0"])
-            V(lambda v: v.memset(T.ex[:, 0:32:2], 0.0), [], ["ex0"])
-            V(lambda v: v.tensor_scalar(T.thr[:, 0:1], T.sm[:, 0:1], -511.5, 512.0, A.mult, A.add), ["sm0"], ["thr"])
-            V(lambda v: v.tensor_tensor(T.yy[:], pick("ii", "lm"), T.tj[:], A.is_gt), ["ii", "lm", "tj2"], ["yy"])
+            V(lambda v: v.tensor_tensor(T.mlo[:], T.mti[:], T.exd[:, 1:32:2], A.min), ["mti", "exd1"], ["mlo"])
+            V(lambda v: v.tensor_tensor(T.mhi[:], T.mti[:], T.exd[:, 1:32:2], A.max), ["mti", "exd1"], ["mhi"])
         if part == 5:
-            V(lambda v: v.tensor_scalar(T.sg[:], T.yy[:], 2.0, -1.0, A.mult, A.add), ["yy"], ["sg"])
+            V(lambda v: v.tensor_copy(L("lmin"), T.mlo[:]), ["mlo"], ["lmin"])
+            V(lambda v: v.tensor_copy(L("lmax"), T.mhi[:]), ["mhi"], ["lmax"])
+            V(lambda v: v.tensor_tensor(T.exd[:, 0:32:2], T.mti[:], T.exd[:, 1:32:2], A.subtract), ["mti", "exd1"], ["exd0"])
 
     flip = [0]
 
@@ -236,16 +256,18 @@ def rank_program(g, core, T, topo):
         return o
 
     def level_list(o, k):
-        V(lambda v: v.tensor_scalar(L("l%d" % k), T[o][:, 15:256:16], col(INV), 1.0, A.mult, A.subtract), [o, "c4"], ["l%d" % k])
+        V(lambda v: v.tensor_scalar(L("l%d" % k), T[o][:, 15:256:16], col("inv"), 1.0, A.mult, A.subtract), [o, "inv"], ["l%d" % k])
 
     def hop(r, k):
         n = n_name(r, k - 1)
         S(lambda s: s.activation(T["n%d" % k][:], pick(n, "l%d" % (k - 1)), F.Copy), [n, "l%d" % (k - 1)], ["n%d" % k])
 
-    def window(src, k):
+    def window(src, k, e):
         b = T.bias[:, 4 + k:5 + k]
-        S(lambda s: s.activation(T.wa[:, 0:128], T[src][:, 0:128], F.Identity, bias=b), [src, "bias"], ["wa.a"])
-        V(lambda v: v.tensor_scalar(T.wa[:, 128:256], T[src][:, 128:256], b, None, A.add), [src, "bias"], ["wa.b"])
+        if e == "s":
+            S(lambda s: s.activation(T.wa[:, 0:CUT], T[src][:, 0:CUT], F.Identity, bias=b), [src, "bias"], ["wa.a"])
+        elif CUT < C:
+            V(lambda v: v.tensor_scalar(T.wa[:, CUT:C], T[src][:, CUT:C], b, None, A.add), [src, "bias"], ["wa.b"])
 
     def grow(out, src, lst):
         V(lambda v: v.tensor_tensor(T[out][:, 0:C], pick("wa", lst), T[src][:, 0:C], A.max), both("wa") + [lst, src], [out])
@@ -256,6 +278,9 @@ def rank_program(g, core, T, topo):
     def unpack(b, pb, out, factor, key, lo=0, n=C):
         S(lambda s: s.activation(T[out][:, C * b + lo:C * b + lo + n], bank(pb, n), F.Copy, scale=factor), ["ps%d" % pb], [key])
 
+    def to_neighbours(name, reads, key, sem):
+        copies([(T[name][16:128, C:2 * C], T[name][0:112, 0:C]), (T[name][0:112, 2 * C:3 * C], T[name][16:128, 0:C])], reads, [key], sem)
+
     for r in range(R3):
         d = STEP[r]
         first = r == 0
@@ -265,135 +290,139 @@ def rank_program(g, core, T, topo):
         lq = ["lq0", "lq1", "lq2c"][r]
         eng = len(few(cores[(rank - d) % len(cores)], core))
         lands(lq, "arq%d" % r, 2 * eng)
-        lands(zp, "arp%d" % r, eng)
-        lands(zb, "arb%d" % r, eng)
+        lands(zp, zp, eng)
+        lands(zb, zb, eng)
         send(to, T[lq][:, 0:C].bitcast(U8), T[qx][:, 0:C].bitcast(U8), "arq%d" % r, both(qx))
         send(to, T[ls][:, 0:C], T[sx][:, 0:C], "arq%d" % r, both(qx))
         for h, s, lo, hi in halves:
             mm(h, ("qu", "su"), 0, (qx, sx), lo, 128, ["qu", "su", qx + s])
         mm(2, ("qu", "su"), 0, (qx, sx), 0, C, ["qu", "su"] + both(qx))
-        if first:
-            o = level_scan(r, 1)
-            more_constants(0)
-            level_list(o, 1)
-            hop(r, 2)
-        for h, s, lo, hi in halves:
-            V(lambda v: v.tensor_tensor(T.wn[:, lo:hi], bank(h, 128), T.cwin[:, lo:hi], A.max), ["ps%d" % h, "cwin"], ["wn" + s])
-        o = level_scan(r, 2)
+        o = level_scan(r, 1)
+        V(lambda v: v.tensor_tensor(T.wn[:, 0:128], bank(0, 128), T.cwin[:, 0:128], A.max), ["ps0", "cwin"], ["wn.a"])
+        level_list(o, 1)
+        hop(r, 2)
+        V(lambda v: v.tensor_tensor(T.wn[:, 128:C], bank(1, 128), T.cwin[:, 128:C], A.max), ["ps1", "cwin"], ["wn.b"])
         V(lambda v: v.tensor_tensor(T.a0[:], pick("wn", "l0"), T.idm[:], A.subtract), both("wn") + ["l0", "idm"], ["a0"])
+        o = level_scan(r, 2)
+        window("a0", 0, "s")
+        window("a0", 0, "v")
         level_list(o, 2)
-        window("a0", 0)
         hop(r, 3)
-        if first:
-            more_constants(1)
-        mm(3, ("qp", "sp"), 0, (qx, sx), 0, C, ["qp", "sp"] + both(qx))
         grow("a1", "a0", "l0")
         if first:
-            more_constants(2)
-        window("a1", 1)
-        S(lambda q: q.activation(T.sw[:, 0:C], bank(2), F.Copy), ["ps2"], ["sw.a"])
+            more_constants(0)
+        window("a1", 1, "s")
         o = level_scan(r, 3)
-        grow("a2", "a1", "l1")
+        window("a1", 1, "v")
         level_list(o, 3)
-        window("a2", 2)
         hop(r, 4)
+        grow("a2", "a1", "l1")
+        window("a2", 2, "s")
         turn(T.n3t[:], T.n3[:], ["n3"], ["n3t"])
-        grow("fw1", "a2", "l2")
-        V(lambda v: v.tensor_tensor(T.tw[:, 288:304], T.n3t[:, 0:256:16], T.cz[:, 1:17], A.subtract), ["n3t", "cz1", "cz2"], ["d8"])
-        turn(T.tw[:, 16:272], T.fw1[:, 0:C], ["fw1"], ["tw"])
+        window("a2", 2, "v")
+        for h, s, lo, hi in halves:
+            V(lambda v: v.tensor_tensor(T.tw[:, 272 * h:272 * h + 8], T.n3t[:, lo:hi:16], T.cz[:, 8 * h:8 * h + 8], A.subtract), ["n3t", "cz0", "cz1"], ["d8" + s])
+        S(lambda q: q.activation(T.sw[:, 0:C], bank(2), F.Copy), ["ps2"], ["sw"])
+        to_neighbours("sw", ["sw"], "swp", "dsw")
+        for h, s, lo, hi in halves:
+            V(lambda v: v.tensor_tensor(T.fw1[:, lo:hi], T.wa[:, 0:C].indirect(L("l2", 8 * h, 8 * h + 8)), T.a2[:, lo:hi], A.max), both("wa") + ["l2", "a2"], ["fw1" + s])
+        S(lambda q: q.activation(T.abf[:], T.fw1[:, 0:C], F.Identity, bias=col("nokey")), both("fw1") + ["nokey"], ["abf"])
+        copies([(T.abf[0:128:16, :], T.idn[0:128:16, :])], ["idn"], ["abf"], "dabf")
+        to_neighbours("fw1", both("fw1"), "fw1p", "dfw1")
+        copies([(T.fw2[0:127, 0:C], T.abf[1:128, :]), (T.fw2[15:128, C:2 * C], T.abf[0:113, :]), (T.fw2[0:111, 2 * C:3 * C], T.abf[17:128, :])], ["abf"], ["fw2"], "dfw2")
+        for h, s, lo, hi in halves:
+            turn(T.tw[:, 16 + lo:16 + hi], T.fw1[:, lo:hi], ["fw1" + s], ["tw" + s])
+            S(lambda q: q.activation(T.yy[:, lo:hi], T.tw[:, 144 * h:144 * h + 144].indirect(L("lc", 8 * h, 8 * h + 8)), F.Copy),
+              ["tw" + s, "tw%d" % h, "d8" + s, "lc" + s], ["yy" + s])
         o = level_scan(r, 4)
-        S(lambda q: q.activation(T.yy[:], pick("tw", "lc", 304), F.Copy), ["tw", "tw0", "tw1", "d8", "lc"], ["yy"])
+        turn(T.b0[:, 0:128], T.yy[:, 0:128], ["yy.a"], ["b0.a"])
         level_list(o, 4)
-        S(lambda q: q.activation(T.abf[:], T.fw1[:, 0:C], F.Identity, bias=col(NOKEY)), ["fw1", "c2"], ["abf"])
-        turn(T.fw1[:, C:544], T.tw[:, 0:288], ["tw", "tw0", "tw1"], ["fw1p"])
+        turn(T.b0[:, 128:C], T.yy[:, 128:C], ["yy.b", "b0.a"], ["b0"])
+        window("b0", 0, "s")
+        window("b0", 0, "v")
         hop(r, 5)
-        turn(T.b0[:], T.yy[:], ["yy"], ["b0"])
-        turn(T.ta[:, 16:272], T.abf[:], ["abf"], ["ta"])
-        window("b0", 0)
-        S(lambda q: q.activation(T.sw[:, C:2 * C], bank(3), F.Copy), ["ps3"], ["sw.b"])
-        V(lambda v: v.tensor_copy(T.ta[:, 32:273:16], T.cz[:, 1:17]), ["cz1", "cz2", "ta"], ["tac"])
-        o = level_scan(r, 5)
+        if first:
+            tiles([2])
         grow("b1", "b0", "l4")
+        window("b1", 1, "s")
+        o = level_scan(r, 5)
+        window("b1", 1, "v")
         level_list(o, 5)
-        window("b1", 1)
         hop(r, 6)
-        turn(T.fw2[:, 0:C], T.ta[:, 17:273], ["ta", "tac"], ["fw2"])
+        if first:
+            more_constants(1)
         grow("b2", "b1", "l5")
-        for b in range(4):
-            if first:
-                V(lambda v: v.quantize_mx(T.qe[:, 128 * b:128 * b + 128], T.se[:, 128 * b:128 * b + 128], T.et[:, 3 - b:515 - b]), ["et"], ["qe%d" % b])
-            if b < 2:
-                mm(b, ("qe", "se"), 128 * b, (qx, sx), 0, C, ["qe%d" % b] + both(qx))
+        window("b2", 2, "s")
+        o = level_scan(r, 6)
+        window("b2", 2, "v")
+        level_list(o, 6)
+        S(lambda q: q.activation(T.s1[:], T.sw[:, 0:C], F.Identity, scale=score, bias=col("keys")), ["sw", "e5", "keys"], ["s1"])
+        if first:
+            more_constants(2)
+            tiles([3])
+        for b in range(2):
+            mm(b, ("qe", "se"), 128 * b, (qx, sx), 0, C, ["qe%d" % b] + both(qx))
         for b in range(4):
             mm(4 + b, ("qe", "se"), 128 * b, (lq, ls), 0, C, ["qe%d" % b, lq])
-        o = level_scan(r, 6)
-        window("b2", 2)
-        level_list(o, 6)
-        S(lambda q: q.activation(T.s1[:], T.sw[:, 0:C], F.Identity, scale=score, bias=col(KEYS)), ["sw.a", "e5", "c1"], ["s1"])
+        grow("b3", "b2", "l6")
+        S(lambda q: q.activation(T.b4[:], T.b3[:], F.Identity, bias=col("nokey")), ["b3", "nokey"], ["b4"])
+        hop(r, 7)
         if first:
             more_constants(3)
-        grow("b3", "b2", "l6")
-        turn(T.fw2[:, C:544], T.ta[:, 1:289], ["ta", "ta0", "tac"], ["fw2p"])
-        hop(r, 7)
+            more_constants(4)
         V(lambda v: v.tensor_tensor(T.od[:], pick("b3", "l3"), T.s1[:], A.subtract), ["b3", "l3", "s1"], ["od"])
-        S(lambda q: q.activation(T.s2[:], pick("sw", "l2s", 512), F.Identity, scale=score, bias=col(EDGE)), both("sw") + ["l2s0", "l2s1", "e5", "c3"], ["s2"])
-        V(lambda v: v.tensor_tensor(T.ev[:], T.b3[:], T.s1[:], A.subtract), ["b3", "s1"], ["ev"])
-        turn(T.xt[:, 0:512:2], T.od[:], ["od"], ["xt0"])
-        S(lambda q: q.activation(T.xt[:, 0:513:32], T.cz[:, 0:17], F.Copy), ["cz0", "cz1", "cz2"], ["xt0"])
-        turn(T.xt[:, 1:512:2], T.ev[:], ["ev"], ["xt1"])
+        V(lambda v: v.tensor_tensor(T.ev[:], T.b4[:], bank(2), A.subtract), ["b4", "ps2"], ["ev"])
+        turn(T.xt[:, :, 0:32:2], T.od[:], ["od"], ["xt0"])
+        turn(T.xt[:, :, 1:32:2], T.ev[:], ["ev"], ["xt1"])
+        S(lambda q: q.activation(T.dd[:], T.xt[:, :, 17:33], F.Copy), ["xt0", "xt1", "xtc"], ["dd"])
+        S(lambda q: q.activation(T.s2[:], pick("sw", "l2s", 768), F.Identity, scale=score, bias=col("edge")), ["sw", "swp", "l2s0", "l2s1", "e5", "edge"], ["s2"])
         o = level_scan(r, 7)
-        unpack(0, 4, "fa", 0.5, "fa.0")
-        unpack(1, 5, "fa", 0.5, "fa.1")
-        V(lambda v: v.tensor_scalar(T.nf2[:, 0:496], T.xt[:, 0:496], 0.0, None, A.is_le), ["xt0", "xt1"], ["nf2"])
-        V(lambda v: v.tensor_scalar(T.sm[:, 8:9], col(INV), -UNIT, None, A.mult), ["c4"], ["sm8"]) if first else None
-        V(lambda v: v.tensor_tensor_scan(T.rc[:, 0:496], T.nf2[:, 0:496], T.xt[:, 17:513], 0.0, A.mult, A.add), ["nf2", "xt0", "xt1"], ["rc"])
-        V(lambda v: v.tensor_scalar(T.dm[:], T[o][:, 15:256:16], T.sm[:, 8:9], None, A.mult), [o, "sm8"], ["dm"])
+        V(lambda v: v.tensor_scalar(T.nf2[:], T.xt[:, :, 0:16], 0.0, None, A.is_le), ["xt0", "xt1"], ["nf2"])
+        V(lambda v: v.tensor_scalar(T.dm[:], T[o][:, 15:256:16], col("ninv"), None, A.mult), [o, "ninv"], ["dm"])
+        V(lambda v: v.tensor_tensor_scan(T.rc[:], T.nf2[:], T.dd[:], 0.0, A.mult, A.add), ["nf2", "dd"], ["rc"])
+        V(lambda v: v.tensor_tensor(T.df[:], T.dm[:], T.ch[:], A.add), ["dm", "ch"], ["df"])
         for e in range(2):
-            V(lambda v: v.tensor_scalar(T.lq2[:, e:16:2], T.rc[:, 15 + 32 * e:496:64], 1.0 / UNIT, col(OFF0 + e), A.mult, A.add), ["rc", "c5", "c6"], ["lq2%d" % e])
-        V(lambda v: v.tensor_tensor(T.df[:], T.dm[:], T.ch[:, 0:16], A.add), ["dm", "ch"], ["df"])
-        S(lambda q: q.activation(T.xr[:], pick("fw2", "lq2", 544), F.Copy), ["fw2", "fw2p", "lq20", "lq21"], ["xr"])
-        V(lambda v: v.tensor_tensor(T.fl[:], pick("fw1", "lq2", 544), T.s2[:], A.is_le), ["fw1", "fw1p", "lq20", "lq21", "s2"], ["fl"])
-        turn(T.rt[:], T.xr[:], ["xr"], ["rt"])
-        S(lambda q: q.activation(T.rt[:, 6:256:16], T.df[:], F.Copy), ["df"], ["rt"])
-        turn(T.zt[:, 16:272], T.fl[:], ["fl"], ["zt"])
-        V(lambda v: v.tensor_tensor_scan(T.rb[:, 0:250], T.zt[:, 15:265], T.rt[:, 6:256], 0.0, A.mult, A.add), ["zt", "zt0", "rt"], ["rb"])
-        S(lambda q: q.activation(T.rt[:, 7:256:16], T.df[:], F.Copy, scale=0.0), ["df"], ["rt"])
-        V(lambda v: v.tensor_scalar(L(lb), T.rb[:, 9:250:16], 1.0 / UNIT, -1.0, A.mult, A.add), ["rb"], [lb])
-        send(to, T[zb][:], L(lb), "arb%d" % r, [lb])
-        V(lambda v: v.tensor_tensor_scan(T.rp[:, 0:249], T.zt[:, 15:264], T.rt[:, 7:256], 0.0, A.mult, A.add), ["zt", "zt0", "rt"], ["rp"])
-        unpack(2, 6, "fa", 0.5, "fa.2")
-        unpack(3, 7, "fa", 0.5, "fa.3")
+            V(lambda v: v.tensor_scalar(L("lq2", e, 16, 2), T.rc[:, 15 + 16 * e:256:32], 1.0 / UNIT, col("off%d" % e), A.mult, A.add), ["rc", "off%d" % e], ["lq2%d" % e])
         if first:
-            V(lambda v: v.tensor_copy(T.tj[:], T.ii[:]), ["ii", "dl"], ["tj", "tj2"])
+            more_constants(5)
+        S(lambda q: q.activation(T.xr[:], pick("fw2", "lq2", 768), F.Copy), ["fw2", "lq20", "lq21"], ["xr"])
+        V(lambda v: v.tensor_tensor(T.fl[:], pick("fw1", "lq2", 768), T.s2[:], A.is_le), both("fw1") + ["fw1p", "lq20", "lq21", "s2"], ["fl"])
+        for b in range(3):
+            unpack(b, 4 + b, "fa", 0.5, "fa.%d" % b)
+        turn(T.rt[:], T.xr[:], ["xr"], ["rt"])
+        turn(T.zt[:, 16:272], T.fl[:], ["fl"], ["zt"])
+        V(lambda v: v.tensor_copy(T.rt[:, 6:256:16], T.df[:]), ["df"], ["rt"])
+        V(lambda v: v.tensor_tensor_scan(T.rb[:, 0:250], T.zt[:, 15:265], T.rt[:, 6:256], 0.0, A.mult, A.add), ["zt", "zt0", "rt"], ["rb"])
+        V(lambda v: v.memset(T.rt[:, 7:256:16], 0.0), [], ["rt"])
+        V(lambda v: v.tensor_scalar(L(lb), T.rb[:, 9:250:16], 1.0 / UNIT, -1.0, A.mult, A.add), ["rb"], [lb])
+        send(to, T[zb][:], L(lb), zb, [lb])
+        V(lambda v: v.tensor_tensor_scan(T.rp[:, 0:249], T.zt[:, 15:264], T.rt[:, 7:256], 0.0, A.mult, A.add), ["zt", "zt0", "rt"], ["rp"])
         V(lambda v: v.tensor_scalar(L(lp), T.rp[:, 8:249:16], 1.0 / UNIT, -1.0, A.mult, A.add), ["rp"], [lp])
-        send(to, T[zp][:], L(lp), "arp%d" % r, [lp])
+        send(to, T[zp][:], L(lp), zp, [lp])
+        S(lambda q: q.activation(T.sb[:], pick("sw", lb), F.Copy), ["sw", lb], ["sb"])
+        S(lambda q: q.activation(T.slo[:, 0:128], T.sb[:, 0:C].indirect(L("lmin", 0, 8)), F.Copy), ["sb", "lmin"], ["slo.a"])
+        V(lambda v: v.tensor_copy(T.slo[:, 128:C], T.sb[:, 0:C].indirect(L("lmin", 8, 16))), ["sb", "lmin"], ["slo.b"])
+        unpack(3, 7, "fa", 0.5, "fa.3")
         for t in (2, 3):
             mm(4 + t, ("qe", "se"), 128 * t, (qx, sx), 0, C, ["qe%d" % t] + both(qx))
-        if first:
-            more_constants(4)
-            more_constants(5)
-        V(lambda v: v.tensor_tensor(T.yn[:], pick("sw", lb), T.sg[:], A.mult), ["sw.a", lb, "sg"], ["yn"])
-        S(lambda q: q.activation(T.yp[:], T.yn[:], F.Copy, scale=-1.0), ["yn"], ["yp"])
+        V(lambda v: v.tensor_tensor(T.xf[:], pick("sb", "lmax"), T.slo[:], A.is_lt), ["sb", "lmax"] + both("slo"), ["xf"])
         unpack(0, 0, "fo", 1.0, "fo.0")
-        unpack(1, 1, "fo", 1.0, "fo.1")
-        V(lambda v: v.tensor_tensor(T.xf[:], pick("yn", "lm"), T.yp[:], A.is_gt), ["yn", "yp", "lm"], ["xf"])
         V(lambda v: v.tensor_tensor_scan(T.xs[:], T.dl[:], T.xf[:], 0.0, A.mult, A.add), ["dl", "xf"], ["xs"])
-        V(lambda v: v.tensor_scalar(T.ex[:, 1:32:2], T.xs[:, 15:256:16], T.thr[:, 0:1], None, A.is_ge), ["xs", "thr"], ["ex1"])
+        V(lambda v: v.tensor_scalar(T.ex[:, 1:32:2], T.xs[:, 15:256:16], col("thr"), None, A.is_ge), ["xs", "thr"], ["ex1"])
         V(lambda v: v.tensor_tensor_scan(T.exo[:], T.ex[:], T.exd[:], 0.0, A.mult, A.add), ["ex0", "ex1", "exd0", "exd1"], ["exo"])
-        V(lambda v: v.tensor_copy(T.lsg[:], T.exo[:, 1:32:2]), ["exo"], ["lsg"])
-        def first_terms(h, s, lo, hi):
+        V(lambda v: v.tensor_copy(L("lsg"), T.exo[:, 1:32:2]), ["exo"], ["lsg"])
+        for h, s, lo, hi in halves:
             for t in range(4):
                 S(lambda q: q.activation(T.zg[:, C * t + lo:C * t + hi], T.fa[:, C * t:C * t + C].indirect(T[zb][:, 8 * h:8 * h + 8]), F.Copy),
                   ["fa.%d" % t, zb], ["zg.%d%s" % (t, s)])
-        first_terms(*halves[0])
-        first_terms(*halves[1])
         old, new = n_name(r, 0), n_name(r + 1, 0)
         if r < 2:
             S(lambda q: q.activation(T[new][:], pick(old, "lsg"), F.Copy), [old, "lsg"], [new])
+        unpack(1, 1, "fo", 1.0, "fo.1")
         def z_ready(h, s, lo, hi):
             quant("qz", "sz", "z", "qz" + s, ["z.%d%s" % (t, s) for t in range(4)], lo)
             for k in range(4):
-                pb = [0, 1, 2, 3, 4, 5, 0, 1][k + 4 * h]
+                pb = [2, 3, 4, 5, 0, 1, 2, 3][k + 4 * h]
                 mm(pb, ("wq", "wp"), 128 * k, ("qz", "sz"), lo, 128, ["wq", "wp", "qz" + s])
                 unpack(k, pb, "hh", 0.03125, "hh.%d%s" % (k, s), lo, 128)
 
@@ -430,11 +459,7 @@ def rank_program(g, core, T, topo):
                 if h == 1 and t == 2:
                     x_ready(*halves[0])
         x_ready(*halves[1])
-        if r < 2:
-            o = level_scan(r + 1, 1)
-            level_list(o, 1)
-            hop(r + 1, 2)
-        else:
+        if r == 2:
             S(lambda q: q.activation(T.a0[:], pick(old, "lsg"), F.Identity, bias=-1.0, scale=1.0 / UNIT), [old, "lsg"], ["a0"])
     op("y", lambda q: q.dma_start(T.nf[:], T.a0[0:128:16, :]), ["a0"], [], "dnf", 16)
     op("y", lambda q: q.dma_start(T.oc[:], T.qx3[:, 0:C].bitcast(U8)), both("qx3"), [], "doc", 16)

from concourse.mybir import dt, AluOpType as A, ActivationFunctionType as F

STEP = [1, 2, 4]
C = 256
R3 = 3
CODE = "float8_e4m3fn_x4"
UNIT = 2.0 ** 80
BIG = 1.0e29
KEY = 1024.0
CUT = 192
LISTS = "l0 l1 l2 l3 l4 l5 l6 lp0 lp1 lp2 lb0 lb1 lb2 lmin lmax lc l2s lq2 lsg ld".split()
SCRATCH = {"ps": ("psum", [128, 4096], "float32"), "xt": ("sbuf", [128, 16, 40], "bfloat16")}
for _names, _cols, _type in [
        ("ut vt", 512, "bfloat16"), ("qu0 qu qv", 128, CODE), ("su0 su sv", 128, "uint8"), ("wq qe", 512, CODE), ("wp se", 512, "uint8"),
        ("ones et", 520, "bfloat16"), ("nxi mti pi ti", 16, "int32"), ("e5 bias cw dm df t16 d16 e16 g16 mlo mhi", 16, "float32"), ("col ex exd exo", 32, "float32"),
        ("ii idm cwin wn wa a0 a1 a2 b0 b1 b2 b3 b4 yy s1 s2 sb slo yt", 256, "float32"), ("sw fw1", 768, "float32"), ("tw", 288, "float32"),
        ("idn dl nsa nsb n3t abf od ev fl xr rt rb rp xf xs nf2 dd rc", 256, "bfloat16"), ("fw2", 768, "bfloat16"), ("zt", 272, "bfloat16"),
        ("cz ch h16", 16, "bfloat16"), ("lu", 16, "uint16"), ("ll", 16 * len(LISTS), "uint16"),
        ("fa fo zg z hh x0 x1 x2 x3", 1024, "bfloat16"), ("qz qx0 qx1 qx2 qx3 lq0 lq1 lq2c", 256, CODE), ("sz sx0 sx1 sx2 sx3 ls0 ls1 ls2", 256, "uint8"),
        ("zp0 zp1 zp2 zb0 zb1 zb2", 16, "uint16"),
        ("f0 f1 n1 n2 n3 n4 n5 n6 n7", 256, "bfloat16")]:
    for _n in _names.split():
        SCRATCH[_n] = ("sbuf", [128, _cols], _type)
DMAS = ["dx", "dnx", "dmt", "du", "dwc", "dws", "dv", "doc", "dos0", "dos1", "dos2", "dos3", "dy0", "dy1", "dnf", "dsw", "dfw1", "dfw2", "dabf"]
SEMAPHORES = ["cv", "cs", "ct", "cg", "sent"] + DMAS + ["%s%d" % (n, i) for n in ("arq", "zp", "zb") for i in range(3)]


def make_issue(g, T):
    queue = {"v": g.vector, "s": g.scalar, "t": g.tensor, "g": g, "y": g.sync}
    known = {e: {} for e in queue}
    count, clock, writer, readers = {}, {}, {}, {}

    def learn(e, ev):
        sem, val = ev
        for s, n in list(clock.get(ev, {}).items()) + [(sem, val)]:
            if known[e].get(s, 0) < n:
                known[e][s] = n

    def need(e, evs):
        best = {}
        for sem, val in evs:
            if known[e].get(sem, 0) < val:
                best[sem] = max(best.get(sem, 0), val)
        evs = [(sem, val) for sem, val in best.items()]
        for ev in evs:
            if not any(o != ev and clock.get(o, {}).get(ev[0], 0) >= ev[1] for o in evs):
                queue[e].wait_ge(T.sem[ev[0]], ev[1])
        for ev in evs:
            learn(e, ev)

    def wait_for(e, reads=(), writes=()):
        evs = []
        for k in reads:
            if k in writer:
                evs.append(writer[k])
            if k.startswith("ps"):
                evs += [ev for ev, o in readers.get(k, []) if o != e]
        for k in writes:
            if k in writer:
                evs.append(writer[k])
            evs += [ev for ev, o in readers.get(k, [])]
        need(e, evs)

    def op(e, calls, reads=(), writes=(), sem=None, inc=1):
        wait_for(e, reads, writes)
        sem = sem or "c" + e
        for call in calls if isinstance(calls, list) else [calls]:
            call(queue[e]).then_inc(T.sem[sem], inc)
            count[sem] = count.get(sem, 0) + inc
        ev = (sem, count[sem])
        clock[ev] = dict(known[e])
        for k in reads:
            readers.setdefault(k, []).append((ev, e))
        for k in writes:
            writer[k] = ev
            readers[k] = []

    def lands(key, sem, val):
        writer[key] = (sem, val)
        readers[key] = []

    return op, wait_for, lands, count


def rank_program(g, core, T, topo):
    rank = T.rank_of(core)
    if rank is None:
        return
    op, wait_for, lands, count = make_issue(g, T)
    cores = T.cores
    U8, U32 = dt.uint8, dt.uint32
    sent = [0]
    halves = [(0, ".a", 0, 128), (1, ".b", 128, 256)]

    def few(src, dst):
        return topo.engines(src, dst)[:8]

    def send(dst, out, src, sem, reads):
        wait_for("g", reads)
        rid, pid = topo.addr(dst)[:2]
        e = few(core, dst)
        g.remote_dma(out, src, T.sem[sem], T.sem.sent, pid, rid, sum(1 << k for k in e))
        sent[0] += len(e)

    def V(call, reads, writes):
        op("v", call, reads, writes)

    def S(call, reads, writes):
        op("s", call, reads, writes)

    def G(call, reads, writes):
        op("g", call, reads, writes)

    def copies(pairs, reads, writes, sem):
        op("y", [(lambda q, o=o, i=i: q.dma_start(o, i)) for o, i in pairs], reads, writes, sem, 16)

    def both(name):
        return [name + ".a", name + ".b"]

    def bank(b, n=C):
        return T.ps[:, 512 * b:512 * b + n]

    def mm(b, stat, c0, mov, lo, n, reads):
        (q, s), (x, y) = stat, mov
        op("t", lambda e: e.matmul_mx(bank(b, n), T[q][:, c0:c0 + 128], T[s][:, c0:c0 + 128], T[x][:, lo:lo + n], T[y][:, lo:lo + n], True, True),
           reads, ["ps%d" % b])

    def quant(q, s, tile, key, reads, lo=0, n=128):
        V(lambda v: v.quantize_mx(T[q][:, lo:lo + n], T[s][:, lo:lo + n], T[tile][:, 4 * lo:4 * lo + 4 * n]), reads, [key])

    def L(lst, a=0, b=16, step=1):
        if lst in LISTS:
            return T.ll[:, 16 * LISTS.index(lst) + a:16 * LISTS.index(lst) + b:step]
        return T[lst][:, a:b]

    def pick(win, lst, n=C):
        return T[win][:, 0:n].indirect(L(lst))

    names = []

    def col(name):
        if name not in names:
            names.append(name)
        return T.col[:, names.index(name):names.index(name) + 1]

    def line(name, src, keys, a, b):
        S(lambda s: s.activation(col(name), src, F.Identity, scale=a, bias=b), keys, [name])

    def whole(out, pattern, base, key):
        G(lambda q: q.iota(out, pattern, base, 0, allow_small_or_imprecise_dtypes=True), [], [key])

    def tiles(which):
        for b in which:
            V(lambda v: v.quantize_mx(T.qe[:, 128 * b:128 * b + 128], T.se[:, 128 * b:128 * b + 128], T.et[:, 3 - b:515 - b]), ["et"], ["qe%d" % b])

    op("y", lambda q: q.dma_start(T.nxi[:], T.nx[:]), [], ["nxi"], "dnx", 16)
    op("s", lambda q: q.dma_start(T.x0[:], T.x[:]), [], ["x0"], "dx", 16)
    op("y", lambda q: q.dma_start(T.ut[:], T.u[:]), [], ["ut"], "du", 16)
    op("y", lambda q: q.dma_start(T.mti[:], T.mt[:]), [], ["mti"], "dmt", 16)

    G(lambda q: q.iota(T.pi[:, 0:1], [[0, 1]], 0, 1), [], ["pi"])
    whole(T.cw[:], [[16, 16]], 0, "k16")
    whole(T.ii[:], [[1, 256]], 1, "ii")
    whole(T.t16[:], [[1, 16]], 0, "t16")
    V(lambda v: v.memset(T.ones[:], 1.0), [], ["ones"])
    G(lambda q: q.affine_select(T.et[:], T.ones[:], [[-1, 520]], A.is_equal, 0.0, 3, 4), ["ones"], ["et"])
    for view, n, key in [(T.tw[:, 8:16], 8, "tw0"), (T.tw[:, 280:288], 8, "tw1"), (T.zt[:, 0:16], 16, "zt0"), (T.ex[:, 0:32:2], 16, "ex0")]:
        whole(view, [[0, n]], 0, key)
    for k, m in enumerate((1, 2, 4, 8, 16, 15, 31)):
        V(lambda v: v.tensor_scalar(T.ti[:, k:k + 1], T.pi[:, 0:1], m, None, A.bitwise_and), ["pi"], ["ti%d" % k])
    ti = ["ti%d" % k for k in range(7)]
    V(lambda v: v.tensor_scalar(T.e5[:, 0:5], T.ti[:, 0:5], 0.0, None, A.is_equal), ti, ["e5"])
    V(lambda v: v.tensor_copy(T.e5[:, 5:7], T.ti[:, 5:7]), ti, ["e8"])
    score, even, lane = T.e5[:, 3:4], T.e5[:, 4:5], T.e5[:, 5:6]
    S(lambda s: s.activation(T.idn[:], T.ii[:], F.Copy, scale=UNIT), ["ii"], ["idn"])
    line("steps", score, ["e5"], -UNIT, UNIT)
    line("low", score, ["e5"], -BIG, 0.0)
    line("key", score, ["e5"], -KEY * UNIT, KEY * UNIT)
    line("i1", T.e5[:, 6:7], ["e8"], UNIT, UNIT)
    S(lambda s: s.activation(T.bias[:, 0:3], T.e5[:, 0:3], F.Identity, scale=BIG, bias=-BIG), ["e5"], ["bias0"])
    line("lc0", score, ["e5"], 15.0 / 16, 1.0 / 16)
    line("lc1", score, ["e5"], 16.0, 0.0)
    line("lc2", score, ["e5"], -248.0, 120.0)
    S(lambda s: s.activation(T.bias[:, 4:7], T.bias[:, 0:3], F.Identity, bias=col("key")), ["bias0", "key"], ["bias"])
    S(lambda s: s.activation(T.bias[:, 8:11], T.e5[:, 0:3], F.Identity, scale=col("key"), accum_out=col("keys0")), ["e5", "key"], ["keys0"])
    V(lambda v: v.tensor_scalar(col("last"), lane, 15.0, None, A.is_equal), ["e8"], ["last"])
    V(lambda v: v.tensor_scalar(T.d16[:], T.t16[:], lane, None, A.subtract), ["t16", "e8"], ["d16"])
    V(lambda v: v.tensor_scalar(L("ld"), T.t16[:], 0.0, lane, A.mult, A.add), ["t16", "e8"], ["ld"])
    V(lambda v: v.tensor_scalar(T.e16[:], T.d16[:], 1.0, 1023.0, A.is_equal, A.mult), ["d16"], ["e16"])
    V(lambda v: v.tensor_scalar(T.g16[:], T.d16[:], 0.0, None, A.not_equal), ["d16"], ["g16"])
    V(lambda v: v.tensor_scalar(T.lu[:, 0:8], T.cw[:, 0:8], 0.0, None, A.add), ["k16"], ["lu"])
    V(lambda v: v.tensor_tensor(T.h16[:], T.e16[:], T.g16[:], A.add), ["e16", "g16"], ["h16"])
    V(lambda v: v.tensor_scalar(T.exd[:, 1:32:2], T.cw[:], lane, None, A.add), ["k16", "e8"], ["exd1"])
    V(lambda v: v.tensor_scalar(col("lane0"), lane, 0.0, -BIG, A.is_equal, A.mult), ["e8"], ["lane0"])
    V(lambda v: v.tensor_copy(L("l0"), T.nxi[:]), ["nxi"], ["l0"])
    V(lambda v: v.tensor_copy(T.dl[:], pick("h16", "ld", 16)), ["h16", "ld"], ["dl"])
    line("inv", col("last"), ["last"], 1023.0 / 1024 / UNIT, 1.0 / 1024 / UNIT)
    line("nokey", col("keys0"), ["keys0"], -1.0, 0.0)
    S(lambda s: s.activation(T.f0[:], pick("idn", "l0"), F.Copy), ["idn", "l0"], ["f0"])
    S(lambda s: s.activation(T.cwin[:], T.ii[:], F.Identity, scale=col("steps"), bias=col("low")), ["ii", "steps", "low"], ["cwin"])
    copies([(T.fw2[:, C * k:C * k + C], T.idn[:]) for k in range(3)], ["idn"], ["fw2"], "dfw2")
    copies([(T.fw1[:, C * k:C * k + C], T.ii[:]) for k in (1, 2)], ["ii"], ["fw1p"], "dfw1")
    copies([(T.sw[:, C * k:C * k + C], T.ii[:]) for k in (1, 2)], ["ii"], ["swp"], "dsw")
    op("y", lambda q: q.dma_start(T.wq[:, 0:512].bitcast(U8), T.wc[:]), [], ["wq"], "dwc", 16)
    op("y", lambda q: q.dma_start(T.wp[:, 0:512], T.ws[:]), [], ["wp"], "dws", 16)
    op("y", lambda q: q.dma_start(T.vt[:], T.v[:]), [], ["vt"], "dv", 16)
    tiles([0])
    quant("qu0", "su0", "ut", "qu0", ["ut"])
    S(lambda s: s.activation(T.n1[:], pick("f0", "l0"), F.Copy), ["f0", "l0"], ["n1"])
    tiles([1])
    V(lambda v: v.tensor_copy(T.qu[:, 0:128].bitcast(U32), T.qu0[:, 0:128].bitcast(U32).indirect(T.lu[:, 0:8])), ["qu0", "lu"], ["qu"])
    S(lambda s: s.activation(T.su[:, 0:128], T.su0[:, 0:128].indirect(T.lu[:, 0:8]), F.Copy), ["qu0", "lu"], ["su"])
    quant("qx0", "sx0", "x0", "qx0.a", ["x0"])
    quant("qx0", "sx0", "x0", "qx0.b", ["x0"], 128)
    S(lambda s: s.activation(T.idm[:], T.ii[:], F.Identity, scale=col("steps")), ["ii", "steps"], ["idm"])

    def more_constants(part):
        if part == 0:
            for e in range(2):
                S(lambda s: s.activation(T.cz[:, e:16:2], T.cw[:, 0:16:2], F.Identity, scale=UNIT, bias=col("i1")), ["k16", "i1"], ["cz%d" % e])
            for h, s, lo, hi in halves:
                V(lambda v: v.tensor_scalar(L("lc", 8 * h, 8 * h + 8), T.cw[:, 8 * h:8 * h + 8], col("lc0"), col("lc%d" % (1 + h)), A.mult, A.add), ["k16", "lc0", "lc1", "lc2"], ["lc" + s])
        if part == 1:
            line("keys", col("keys0"), ["keys0", "lane0"], 1.0, col("lane0"))
            line("edge0", col("last"), ["last"], -2.0 * BIG / UNIT, BIG / UNIT)
            line("w0", even, ["e5"], -272.0, 272.0)
            line("w1", even, ["e5"], 496.0, 0.0)
        if part == 2:
            line("edge", col("edge0"), ["edge0", "steps"], col("steps"), 0.0)
            line("off0", even, ["e5"], -256.0, 255.0)
            line("off1", even, ["e5"], 512.0, -1.0)
            line("ninv", col("inv"), ["inv"], -UNIT, 0.0)
            for e in range(2):
                V(lambda v: v.tensor_scalar(L("l2s", e, 16, 2), T.cw[:, e:16:2], col("w%d" % e), lane, A.add, A.add), ["k16", "w%d" % e, "e8"], ["l2s%d" % e])
        if part == 3:
            S(lambda s: s.activation(T.xt[:, :, 32], T.cz[:], F.Copy), ["cz0", "cz1"], ["xtc"])
            S(lambda s: s.activation(T.ch[:], T.exd[:, 1:32:2], F.Identity, scale=UNIT, bias=UNIT), ["exd1"], ["ch"])
            line("thr", col("last"), ["last"], -511.5, 512.0)
        if part == 4:
            V(lambda v: v.tensor_tensor(T.mlo[:], T.mti[:], T.exd[:, 1:32:2], A.min), ["mti", "exd1"], ["mlo"])
            V(lambda v: v.tensor_tensor(T.mhi[:], T.mti[:], T.exd[:, 1:32:2], A.max), ["mti", "exd1"], ["mhi"])
        if part == 5:
            V(lambda v: v.tensor_copy(L("lmin"), T.mlo[:]), ["mlo"], ["lmin"])
            V(lambda v: v.tensor_copy(L("lmax"), T.mhi[:]), ["mhi"], ["lmax"])
            V(lambda v: v.tensor_tensor(T.exd[:, 0:32:2], T.mti[:], T.exd[:, 1:32:2], A.subtract), ["mti", "exd1"], ["exd0"])

    flip = [0]

    def n_name(r, k):
        return "f%d" % (r % 2) if k == 0 else "n%d" % k

    def level_scan(r, k):
        flip[0] ^= 1
        o, n = ["nsa", "nsb"][flip[0]], n_name(r, k)
        V(lambda v: v.tensor_tensor_scan(T[o][:], T.dl[:], T[n][:], 0.0, A.mult, A.max), ["dl", n], [o])
        return o

    def level_list(o, k):
        V(lambda v: v.tensor_scalar(L("l%d" % k), T[o][:, 15:256:16], col("inv"), 1.0, A.mult, A.subtract), [o, "inv"], ["l%d" % k])

    def hop(r, k):
        n = n_name(r, k - 1)
        S(lambda s: s.activation(T["n%d" % k][:], pick(n, "l%d" % (k - 1)), F.Copy), [n, "l%d" % (k - 1)], ["n%d" % k])

    def window(src, k, e):
        b = T.bias[:, 4 + k:5 + k]
        if e == "s":
            S(lambda s: s.activation(T.wa[:, 0:CUT], T[src][:, 0:CUT], F.Identity, bias=b), [src, "bias"], ["wa.a"])
        elif CUT < C:
            V(lambda v: v.tensor_scalar(T.wa[:, CUT:C], T[src][:, CUT:C], b, None, A.add), [src, "bias"], ["wa.b"])

    def grow(out, src, lst):
        V(lambda v: v.tensor_tensor(T[out][:, 0:C], pick("wa", lst), T[src][:, 0:C], A.max), both("wa") + [lst, src], [out])

    def turn(out, src, reads, writes):
        V(lambda v: v.transpose(out, src), reads, writes)

    def unpack(b, pb, out, factor, key, lo=0, n=C):
        S(lambda s: s.activation(T[out][:, C * b + lo:C * b + lo + n], bank(pb, n), F.Copy, scale=factor), ["ps%d" % pb], [key])

    def to_neighbours(name, reads, key, sem):
        copies([(T[name][16:128, C:2 * C], T[name][0:112, 0:C]), (T[name][0:112, 2 * C:3 * C], T[name][16:128, 0:C])], reads, [key], sem)

    for r in range(R3):
        d = STEP[r]
        first = r == 0
        to = cores[(rank + d) % len(cores)]
        qx, sx = "qx%d" % r, "sx%d" % r
        ls, zp, zb, lp, lb = ["%s%d" % (n, r) for n in ("ls", "zp", "zb", "lp", "lb")]
        lq = ["lq0", "lq1", "lq2c"][r]
        eng = len(few(cores[(rank - d) % len(cores)], core))
        lands(lq, "arq%d" % r, 2 * eng)
        lands(zp, zp, eng)
        lands(zb, zb, eng)
        send(to, T[lq][:, 0:C].bitcast(U8), T[qx][:, 0:C].bitcast(U8), "arq%d" % r, both(qx))
        send(to, T[ls][:, 0:C], T[sx][:, 0:C], "arq%d" % r, both(qx))
        for h, s, lo, hi in halves:
            mm(h, ("qu", "su"), 0, (qx, sx), lo, 128, ["qu", "su", qx + s])
        mm(2, ("qu", "su"), 0, (qx, sx), 0, C, ["qu", "su"] + both(qx))
        o = level_scan(r, 1)
        V(lambda v: v.tensor_tensor(T.wn[:, 0:128], bank(0, 128), T.cwin[:, 0:128], A.max), ["ps0", "cwin"], ["wn.a"])
        level_list(o, 1)
        hop(r, 2)
        V(lambda v: v.tensor_tensor(T.wn[:, 128:C], bank(1, 128), T.cwin[:, 128:C], A.max), ["ps1", "cwin"], ["wn.b"])
        V(lambda v: v.tensor_tensor(T.a0[:], pick("wn", "l0"), T.idm[:], A.subtract), both("wn") + ["l0", "idm"], ["a0"])
        o = level_scan(r, 2)
        window("a0", 0, "s")
        window("a0", 0, "v")
        level_list(o, 2)
        hop(r, 3)
        grow("a1", "a0", "l0")
        if first:
            more_constants(0)
        window("a1", 1, "s")
        o = level_scan(r, 3)
        window("a1", 1, "v")
        level_list(o, 3)
        hop(r, 4)
        grow("a2", "a1", "l1")
        window("a2", 2, "s")
        turn(T.n3t[:], T.n3[:], ["n3"], ["n3t"])
        window("a2", 2, "v")
        for h, s, lo, hi in halves:
            V(lambda v: v.tensor_tensor(T.tw[:, 272 * h:272 * h + 8], T.n3t[:, lo:hi:16], T.cz[:, 8 * h:8 * h + 8], A.subtract), ["n3t", "cz0", "cz1"], ["d8" + s])
        S(lambda q: q.activation(T.sw[:, 0:C], bank(2), F.Copy), ["ps2"], ["sw"])
        to_neighbours("sw", ["sw"], "swp", "dsw")
        for h, s, lo, hi in halves:
            V(lambda v: v.tensor_tensor(T.fw1[:, lo:hi], T.wa[:, 0:C].indirect(L("l2", 8 * h, 8 * h + 8)), T.a2[:, lo:hi], A.max), both("wa") + ["l2", "a2"], ["fw1" + s])
        S(lambda q: q.activation(T.abf[:], T.fw1[:, 0:C], F.Identity, bias=col("nokey")), both("fw1") + ["nokey"], ["abf"])
        copies([(T.abf[0:128:16, :], T.idn[0:128:16, :])], ["idn"], ["abf"], "dabf")
        to_neighbours("fw1", both("fw1"), "fw1p", "dfw1")
        copies([(T.fw2[0:127, 0:C], T.abf[1:128, :]), (T.fw2[15:128, C:2 * C], T.abf[0:113, :]), (T.fw2[0:111, 2 * C:3 * C], T.abf[17:128, :])], ["abf"], ["fw2"], "dfw2")
        for h, s, lo, hi in halves:
            turn(T.tw[:, 16 + lo:16 + hi], T.fw1[:, lo:hi], ["fw1" + s], ["tw" + s])
            S(lambda q: q.activation(T.yy[:, lo:hi], T.tw[:, 144 * h:144 * h + 144].indirect(L("lc", 8 * h, 8 * h + 8)), F.Copy),
              ["tw" + s, "tw%d" % h, "d8" + s, "lc" + s], ["yy" + s])
        o = level_scan(r, 4)
        turn(T.b0[:, 0:128], T.yy[:, 0:128], ["yy.a"], ["b0.a"])
        level_list(o, 4)
        turn(T.b0[:, 128:C], T.yy[:, 128:C], ["yy.b", "b0.a"], ["b0"])
        window("b0", 0, "s")
        window("b0", 0, "v")
        hop(r, 5)
        if first:
            tiles([2])
        grow("b1", "b0", "l4")
        window("b1", 1, "s")
        o = level_scan(r, 5)
        window("b1", 1, "v")
        level_list(o, 5)
        hop(r, 6)
        if first:
            more_constants(1)
        grow("b2", "b1", "l5")
        window("b2", 2, "s")
        o = level_scan(r, 6)
        window("b2", 2, "v")
        level_list(o, 6)
        S(lambda q: q.activation(T.s1[:], T.sw[:, 0:C], F.Identity, scale=score, bias=col("keys")), ["sw", "e5", "keys"], ["s1"])
        if first:
            more_constants(2)
            tiles([3])
        for b in range(2):
            mm(b, ("qe", "se"), 128 * b, (qx, sx), 0, C, ["qe%d" % b] + both(qx))
        for b in range(4):
            mm(4 + b, ("qe", "se"), 128 * b, (lq, ls), 0, C, ["qe%d" % b, lq])
        grow("b3", "b2", "l6")
        S(lambda q: q.activation(T.b4[:], T.b3[:], F.Identity, bias=col("nokey")), ["b3", "nokey"], ["b4"])
        hop(r, 7)
        if first:
            more_constants(3)
            more_constants(4)
        V(lambda v: v.tensor_tensor(T.od[:], pick("b3", "l3"), T.s1[:], A.subtract), ["b3", "l3", "s1"], ["od"])
        V(lambda v: v.tensor_tensor(T.ev[:], T.b4[:], bank(2), A.subtract), ["b4", "ps2"], ["ev"])
        turn(T.xt[:, :, 0:32:2], T.od[:], ["od"], ["xt0"])
        turn(T.xt[:, :, 1:32:2], T.ev[:], ["ev"], ["xt1"])
        S(lambda q: q.activation(T.dd[:], T.xt[:, :, 17:33], F.Copy), ["xt0", "xt1", "xtc"], ["dd"])
        S(lambda q: q.activation(T.s2[:], pick("sw", "l2s", 768), F.Identity, scale=score, bias=col("edge")), ["sw", "swp", "l2s0", "l2s1", "e5", "edge"], ["s2"])
        o = level_scan(r, 7)
        V(lambda v: v.tensor_scalar(T.nf2[:], T.xt[:, :, 0:16], 0.0, None, A.is_le), ["xt0", "xt1"], ["nf2"])
        V(lambda v: v.tensor_scalar(T.dm[:], T[o][:, 15:256:16], col("ninv"), None, A.mult), [o, "ninv"], ["dm"])
        V(lambda v: v.tensor_tensor_scan(T.rc[:], T.nf2[:], T.dd[:], 0.0, A.mult, A.add), ["nf2", "dd"], ["rc"])
        V(lambda v: v.tensor_tensor(T.df[:], T.dm[:], T.ch[:], A.add), ["dm", "ch"], ["df"])
        for e in range(2):
            V(lambda v: v.tensor_scalar(L("lq2", e, 16, 2), T.rc[:, 15 + 16 * e:256:32], 1.0 / UNIT, col("off%d" % e), A.mult, A.add), ["rc", "off%d" % e], ["lq2%d" % e])
        if first:
            more_constants(5)
        S(lambda q: q.activation(T.xr[:], pick("fw2", "lq2", 768), F.Copy), ["fw2", "lq20", "lq21"], ["xr"])
        V(lambda v: v.tensor_tensor(T.fl[:], pick("fw1", "lq2", 768), T.s2[:], A.is_le), both("fw1") + ["fw1p", "lq20", "lq21", "s2"], ["fl"])
        for b in range(3):
            unpack(b, 4 + b, "fa", 0.5, "fa.%d" % b)
        turn(T.rt[:], T.xr[:], ["xr"], ["rt"])
        turn(T.zt[:, 16:272], T.fl[:], ["fl"], ["zt"])
        V(lambda v: v.tensor_copy(T.rt[:, 6:256:16], T.df[:]), ["df"], ["rt"])
        V(lambda v: v.tensor_tensor_scan(T.rb[:, 0:250], T.zt[:, 15:265], T.rt[:, 6:256], 0.0, A.mult, A.add), ["zt", "zt0", "rt"], ["rb"])
        V(lambda v: v.memset(T.rt[:, 7:256:16], 0.0), [], ["rt"])
        V(lambda v: v.tensor_scalar(L(lb), T.rb[:, 9:250:16], 1.0 / UNIT, -1.0, A.mult, A.add), ["rb"], [lb])
        send(to, T[zb][:], L(lb), zb, [lb])
        V(lambda v: v.tensor_tensor_scan(T.rp[:, 0:249], T.zt[:, 15:264], T.rt[:, 7:256], 0.0, A.mult, A.add), ["zt", "zt0", "rt"], ["rp"])
        V(lambda v: v.tensor_scalar(L(lp), T.rp[:, 8:249:16], 1.0 / UNIT, -1.0, A.mult, A.add), ["rp"], [lp])
        send(to, T[zp][:], L(lp), zp, [lp])
        S(lambda q: q.activation(T.sb[:], pick("sw", lb), F.Copy), ["sw", lb], ["sb"])
        S(lambda q: q.activation(T.slo[:, 0:128], T.sb[:, 0:C].indirect(L("lmin", 0, 8)), F.Copy), ["sb", "lmin"], ["slo.a"])
        V(lambda v: v.tensor_copy(T.slo[:, 128:C], T.sb[:, 0:C].indirect(L("lmin", 8, 16))), ["sb", "lmin"], ["slo.b"])
        unpack(3, 7, "fa", 0.5, "fa.3")
        for t in (2, 3):
            mm(4 + t, ("qe", "se"), 128 * t, (qx, sx), 0, C, ["qe%d" % t] + both(qx))
        V(lambda v: v.tensor_tensor(T.xf[:], pick("sb", "lmax"), T.slo[:], A.is_lt), ["sb", "lmax"] + both("slo"), ["xf"])
        unpack(0, 0, "fo", 1.0, "fo.0")
        V(lambda v: v.tensor_tensor_scan(T.xs[:], T.dl[:], T.xf[:], 0.0, A.mult, A.add), ["dl", "xf"], ["xs"])
        V(lambda v: v.tensor_scalar(T.ex[:, 1:32:2], T.xs[:, 15:256:16], col("thr"), None, A.is_ge), ["xs", "thr"], ["ex1"])
        V(lambda v: v.tensor_tensor_scan(T.exo[:], T.ex[:], T.exd[:], 0.0, A.mult, A.add), ["ex0", "ex1", "exd0", "exd1"], ["exo"])
        V(lambda v: v.tensor_copy(L("lsg"), T.exo[:, 1:32:2]), ["exo"], ["lsg"])
        for h, s, lo, hi in halves:
            for t in range(4):
                S(lambda q: q.activation(T.zg[:, C * t + lo:C * t + hi], T.fa[:, C * t:C * t + C].indirect(T[zb][:, 8 * h:8 * h + 8]), F.Copy),
                  ["fa.%d" % t, zb], ["zg.%d%s" % (t, s)])
        old, new = n_name(r, 0), n_name(r + 1, 0)
        if r < 2:
            S(lambda q: q.activation(T[new][:], pick(old, "lsg"), F.Copy), [old, "lsg"], [new])
        unpack(1, 1, "fo", 1.0, "fo.1")
        def z_ready(h, s, lo, hi):
            quant("qz", "sz", "z", "qz" + s, ["z.%d%s" % (t, s) for t in range(4)], lo)
            for k in range(4):
                pb = [2, 3, 4, 5, 0, 1, 2, 3][k + 4 * h]
                mm(pb, ("wq", "wp"), 128 * k, ("qz", "sz"), lo, 128, ["wq", "wp", "qz" + s])
                unpack(k, pb, "hh", 0.03125, "hh.%d%s" % (k, s), lo, 128)

        for h, s, lo, hi in halves:
            for t in range(4):
                V(lambda v: v.tensor_tensor(T.z[:, 4 * lo + t:4 * hi:4], T.fa[:, C * t:C * t + C].indirect(T[zp][:, 8 * h:8 * h + 8]), T.zg[:, C * t + lo:C * t + hi], A.add),
                  ["fa.%d" % t, zp, "zg.%d%s" % (t, s)], ["z.%d%s" % (t, s)])
                if h == 1 and t == 0:
                    z_ready(*halves[0])
        z_ready(*halves[1])
        if r < 2:
            o = level_scan(r + 1, 0)
            level_list(o, 0)
        else:
            quant("qv", "sv", "vt", "qv", ["vt"])
        xn = "x%d" % (r + 1)
        def x_ready(h, s, lo, hi):
            quant("qx%d" % (r + 1), "sx%d" % (r + 1), xn, "qx%d%s" % (r + 1, s), ["%s.%d%s" % (xn, t, s) for t in range(4)], lo)

        for h, s, lo, hi in halves:
            for t in (2, 3):
                S(lambda q: q.activation(T.zg[:, C * t + lo:C * t + hi], T.hh[:, C * t:C * t + C].indirect(L(lb, 8 * h, 8 * h + 8)), F.Copy),
                  both("hh.%d" % t) + [lb], ["zg.%d%s" % (t, s)])
        if r < 2:
            hop(r + 1, 1)
        for h, s, lo, hi in halves:
            for t in (0, 1):
                V(lambda v: v.tensor_tensor(T[xn][:, 4 * lo + t:4 * hi:4], T.hh[:, C * t:C * t + C].indirect(L(lb, 8 * h, 8 * h + 8)), T.fo[:, C * t + lo:C * t + hi], A.add),
                  both("hh.%d" % t) + ["fo.%d" % t, lb], ["%s.%d%s" % (xn, t, s)])
        for h, s, lo, hi in halves:
            for t in (2, 3):
                V(lambda v: v.tensor_tensor(T[xn][:, 4 * lo + t:4 * hi:4], T.zg[:, C * t + lo:C * t + hi], T.ps[:, 512 * (4 + t) + lo:512 * (4 + t) + hi], A.add),
                  ["zg.%d%s" % (t, s), "ps%d" % (4 + t)], ["%s.%d%s" % (xn, t, s)])
                if h == 1 and t == 2:
                    x_ready(*halves[0])
        x_ready(*halves[1])
        if r == 2:
            S(lambda q: q.activation(T.a0[:], pick(old, "lsg"), F.Identity, bias=-1.0, scale=1.0 / UNIT), [old, "lsg"], ["a0"])
    op("y", lambda q: q.dma_start(T.nf[:], T.a0[0:128:16, :]), ["a0"], [], "dnf", 16)
    op("y", lambda q: q.dma_start(T.oc[:], T.qx3[:, 0:C].bitcast(U8)), both("qx3"), [], "doc", 16)
    for h in range(2):
        mm(6 + h, ("qv", "sv"), 0, ("qx3", "sx3"), 128 * h, 128, ["qv", "qx3" + [".a", ".b"][h]])
    V(lambda v: v.tensor_copy(T.yt[:, 0:128], bank(6, 128)), ["ps6"], ["yt.0"])
    for k in range(2):
        op("s", lambda q: q.dma_start(T.osc[4 * k:4 * k + 4, 0:C], T.sx3[32 * k:32 * k + 4, 0:C]), both("qx3"), [], "dos%d" % k, 16)
    S(lambda s: s.activation(T.yt[:, 128:256], bank(7, 128), F.Copy), ["ps7"], ["yt.1"])
    op("y", lambda q: q.dma_start(T.y[:, 0:128], T.yt[:, 0:128]), ["yt.0"], [], "dy0", 16)
    op("s", lambda q: q.dma_start(T.y[:, 128:256], T.yt[:, 128:256]), ["yt.1"], [], "dy1", 16)
    for k in range(2, 4):
        op("y", lambda q: q.dma_start(T.osc[4 * k:4 * k + 4, 0:C], T.sx3[32 * k:32 * k + 4, 0:C]), both("qx3"), [], "dos%d" % k, 16)
    for s, n in count.items():
        g.wait_ge(T.sem[s], n)
    g.wait_ge(T.sem.sent, sent[0])
